import numpy as np
import ml_dtypes


def mxq(x, axis, fmt="e4m3"):
    dtype, down = {"e4m3": (ml_dtypes.float8_e4m3fn, 7), "e5m2": (ml_dtypes.float8_e5m2, 14)}[fmt]
    v = np.moveaxis(np.asarray(x, np.float32).astype(ml_dtypes.bfloat16).astype(np.float64), axis, -1)
    blocks = v.reshape(v.shape[:-1] + (-1, 32))
    amax = np.abs(blocks).max(-1, keepdims=True)
    byte = np.maximum(np.where(amax > 0, np.frexp(amax)[1] - 1 + 127, 0) - down, 1)
    scale = np.exp2(byte - 127.0)
    codes = (blocks / scale).astype(np.float32).astype(dtype).astype(np.float64)
    return np.moveaxis((codes * scale).reshape(v.shape), -1, axis)


WIDE = False


def mx_kscale(k):
    if not WIDE:
        return np.ones(k)
    levels = np.array([10, -10, 5, -5, 0])
    if k % 512:
        return np.exp2(np.random.permutation(np.resize(levels, k // 32))).repeat(32)
    a = np.empty((k // 512, 16))
    for p in range(k // 512):
        a[p, :8] = np.random.permutation(np.resize(levels, 8))
        for g in range(8):
            far = levels[np.abs(levels - a[p, g]) >= 10]
            a[p, g + 8] = far[np.random.randint(len(far))]
    return np.exp2(a.ravel()).repeat(32)


def f64(x):
    return np.asarray(x).astype(np.float64)


def striped(idx):
    return np.tile(idx.reshape(-1, 16).T, (8, 1)).astype(np.uint16)


def unstriped(offs):
    return offs[:16].T.reshape(-1).astype(np.int64)


E2M1 = np.array([0.0, 0.5, 1.0, 1.5, 2.0, 3.0, 4.0, 6.0, -0.0, -0.5, -1.0, -1.5, -2.0, -3.0, -4.0, -6.0])


def pack_weight(w, fmt):
    k, n = w.shape
    w = f64(np.asarray(w, np.float32).astype(ml_dtypes.bfloat16)).reshape(k // 32, 32, n)
    amax = np.abs(w).max(1)
    if fmt == "e4m3":
        byte = np.frexp(amax)[1] - 1 + 127 - 7
    else:
        mant, ex = np.frexp(amax / 6.0)
        byte = np.where(mant > 0.5, ex, ex - 1) + 127
    byte = np.clip(np.where(amax > 0, byte, 1), 1, 254)
    scaled = (w * np.exp2(127.0 - byte)[:, None, :]).reshape(k, n).astype(np.float32)
    by_word = np.ascontiguousarray(scaled.reshape(k // 512, 128, 4, n).transpose(0, 1, 3, 2))
    if fmt == "e4m3":
        words = by_word.astype(ml_dtypes.float8_e4m3fn).view(np.uint8)
    else:
        c = by_word.astype(ml_dtypes.float4_e2m1fn).view(np.uint8) & 0xF
        words = (c[..., 0::2] | (c[..., 1::2] << 4)).reshape(k // 512, 128, 2 * n)
    return np.ascontiguousarray(words), np.ascontiguousarray(byte.astype(np.uint8).reshape(k // 512, 16, n))


def unpack_weight(words, scales, fmt):
    g, _, n = scales.shape
    words = np.ascontiguousarray(words).reshape(g, 128, n, -1)
    if fmt == "e4m3":
        vals = words.view(ml_dtypes.float8_e4m3fn).astype(np.float64)
    else:
        nib = np.empty((g, 128, n, 4), np.uint8)
        nib[..., 0::2] = words & 0xF
        nib[..., 1::2] = words >> 4
        vals = E2M1[nib]
    vals = vals * np.repeat(np.exp2(scales.astype(np.float64) - 127.0), 8, axis=1)[..., None]
    return vals.transpose(0, 1, 3, 2).reshape(g * 512, n)


def relu(v):
    return np.maximum(v, 0.0)


K, T, E, C, N = 2048, 512, 4, 256, 128


def by_expert(wq, xq):
    return np.concatenate([wq[e].T @ xq[:, e * C:(e + 1) * C] for e in range(E)], axis=1)


def setup_inputs():
    n = np.random.standard_normal
    s = mx_kscale(K)[:, None]
    first = np.random.permutation(np.repeat(np.arange(E), T // E))
    second = (first + 1 + np.random.permutation(np.repeat(np.arange(E - 1), -(-T // (E - 1)))[:T])) % E
    while np.bincount(second, minlength=E).max() != T // E:
        load = np.bincount(second, minlength=E); hi, lo = int(load.argmax()), int(load.argmin())
        t = np.flatnonzero((second == hi) & (first != lo))[0]; second[t] = lo
    slot_token = np.empty(E * C, np.int64); pos = np.empty((2, T), np.int64); fill = np.zeros(E, np.int64)
    place = np.stack([np.random.permutation(C) for _ in range(E)])
    for r, deal in enumerate((first, second)):
        for t in np.random.permutation(T):
            e = deal[t]; j = e * C + place[e, fill[e]]; fill[e] += 1; slot_token[j] = t; pos[r, t] = j
    g = np.random.uniform(0.2, 0.8, T)
    w = [pack_weight(m, "e2m1") for m in n((E + 1, K, N)) / np.sqrt(K) / s[None]]
    return {
        "xT": (n((K, T)) * s).astype(np.float32),
        "w_words": np.stack([m[0] for m in w]),
        "w_scales": np.stack([m[1] for m in w]),
        "b": (0.3 * n((N, E + 1))).astype(np.float32),
        "gate": np.stack([np.tile(g, (N, 1)), np.tile(1.0 - g, (N, 1))]).astype(np.float32),
        "offs": striped(slot_token),
        "pos1": striped(pos[0]),
        "pos2": striped(pos[1]),
    }


def reference(xT, w_words, w_scales, b, gate, offs, pos1, pos2):
    idx = unstriped(offs)
    w = np.stack([unpack_weight(w_words[e], w_scales[e], "e2m1") for e in range(E + 1)])
    wq = w
    xs = mxq(f64(xT), 0, "e4m3")
    ys = relu((wq[E].T @ xs) + f64(b)[:, E:])
    xq = mxq(f64(xT)[:, idx], 0, "e4m3")
    y = by_expert(w, xq)
    y = relu(y + np.repeat(f64(b)[:, :E], C, axis=1))
    return ys + f64(gate[0]) * y[:, unstriped(pos1)] + f64(gate[1]) * y[:, unstriped(pos2)]

@@ -1,0 +1,207 @@
+from contextlib import ExitStack
+
+import concourse.mybir as mybir
+
+F32 = mybir.dt.float32
+BF16 = mybir.dt.bfloat16
+U32 = mybir.dt.uint32
+I32 = mybir.dt.int32
+U16 = mybir.dt.uint16
+U8 = mybir.dt.uint8
+FP8X4 = mybir.dt.float8_e4m3fn_x4
+FP4X4 = mybir.dt.float4_e2m1fn_x4
+RELU = mybir.ActivationFunctionType.Relu
+COPY = mybir.ActivationFunctionType.Copy
+MULT = mybir.AluOpType.mult
+
+P = 128
+K, T, E, C, N = 2048, 512, 4, 256, 128
+K_PASS = 512
+PASSES = K // K_PASS
+LAST = PASSES - 1
+SLOTS = E * C
+PIECES = {1: ((0, 384), (384, 768), (768, 1024)), 2: ((0, 768), (768, 1024)), 3: ((0, 1024),)}
+
+FLOPS = 2 * K * N * (SLOTS + T)
+
+
+def tile_moe_shr_lin_relu_kernel(tc, xT, w_words, w_scales, b, gate, offs, pos1, pos2, out):
+    nc = tc.nc
+    with ExitStack() as ctx:
+        keep = ctx.enter_context(tc.tile_pool(name="keep", bufs=1))
+        psum = ctx.enter_context(tc.psum_pool(name="psum", bufs=1))
+
+        offs_sb = keep.tile([P, SLOTS // 16], U16, name="offs_sb")
+        pos1_sb = keep.tile([P, T // 16], U16, name="pos1_sb")
+        pos2_sb = keep.tile([P, T // 16], U16, name="pos2_sb")
+        w_sb = keep.tile([P, (E + 1) * PASSES, 2 * N], U8, name="w_sb", align_bytes=64)
+        ws_sb = keep.tile([P, (E + 1) * PASSES, N], U8, name="ws_sb", align_bytes=64)
+        b_sb = keep.tile([P, E + 1], F32, name="b_sb")
+        gate_sb = keep.tile([P, 2, T], F32, name="gate_sb")
+        y_sb = keep.tile([P, SLOTS], F32, name="y_sb")
+        ys_sb = keep.tile([P, T], F32, name="ys_sb")
+        planes = keep.tile([P, 4, T], BF16, name="planes", align_bytes=64)
+        banks = [psum.tile([P, N], F32, name=f"bank{i}", tag=f"bank{i}") for i in range(8)]
+        first_pairs = keep.tile([P, 2, T, 2], BF16, name="first_pairs", align_bytes=64)
+        more_pairs = keep.tile([P, 4, T, 2], BF16, name="more_pairs", align_bytes=64)
+        pairs = {0: first_pairs[:], 1: more_pairs[:, 0:2], 2: more_pairs[:, 2:4]}
+        windows = {(0, 0): first_pairs[:, 0:1], (0, 1): first_pairs[:, 1:2]}
+        for s in range(4):
+            windows[1 + s // 2, s % 2] = more_pairs[:, s : min(s + 3, 4)]
+        raw, gath, q_in, codes, scales = {}, {}, {}, {}, {}
+        for a in range(PASSES):
+            raw[a] = keep.tile([P, 4, T], F32, name=f"raw_{a}")
+            codes[a] = keep.tile([P, SLOTS], U32, name=f"codes_{a}", align_bytes=64)
+            scales[a] = keep.tile([P, SLOTS], U8, name=f"scales_{a}", align_bytes=64)
+            q_in[a] = keep.tile([P, SLOTS, 4], BF16, name=f"q_in_{a}", align_bytes=64)
+            if a != LAST:
+                gath[a] = keep.tile([P, 2, SLOTS, 2], BF16, name=f"gath_{a}", align_bytes=64)
+
+        nc.vector.memset(ws_sb[:].rearrange("p g n -> p (g n)").bitcast(I32), 0)
+
+        for a in range(PASSES):
+            rows = xT[a * K_PASS : (a + 1) * K_PASS, :].rearrange("(p u e) w -> u p e w", u=2, e=2)
+            for u in range(2):
+                nc.sync.dma_start(raw[a][:, 2 * u : 2 * u + 2], rows[u])
+                if a == 0 and u == 0:
+                    nc.sync.dma_start(offs_sb[:], offs)
+        nc.sync.dma_start(w_sb[:].bitcast(I32), w_words.rearrange("e a p n -> p (e a) n").bitcast(I32))
+        scale_rows = w_scales.rearrange("e a q n -> q (e a) n").bitcast(I32)
+        for quad in range(4):
+            nc.sync.dma_start(ws_sb[32 * quad : 32 * quad + 4].bitcast(I32), scale_rows[4 * quad : 4 * quad + 4])
+        nc.sync.dma_start(b_sb[:], b)
+        nc.sync.dma_start(pos1_sb[:], pos1)
+        nc.sync.dma_start(pos2_sb[:], pos2)
+        nc.sync.dma_start(gate_sb[:], gate.rearrange("r n t -> n r t"))
+
+        def cast(a, u, lo, hi, copy):
+            copy(pairs[a][:, u, lo:hi], raw[a][:, 2 * u : 2 * u + 2, lo:hi].rearrange("p e w -> p w e"))
+
+        def gather(a, u):
+            window = windows[a, u]
+            for lo, hi in PIECES[window.shape[1]]:
+                nc.vector.tensor_copy(
+                    gath[a][:, u, lo:hi].rearrange("p n e -> p (n e)").bitcast(U32),
+                    window.rearrange("p s w e -> p (s w e)").bitcast(U32).indirect(offs_sb[:, lo // 16 : hi // 16]),
+                )
+
+        def interleave(a):
+            nc.vector.tensor_copy(
+                q_in[a][:].rearrange("p n (u e) -> p n u e", u=2), gath[a][:].rearrange("p u n e -> p n u e")
+            )
+
+        def quantize(a, lo, hi):
+            nc.vector.quantize_mx(
+                out=codes[a][:, lo:hi].bitcast(FP8X4),
+                scales=scales[a][:, lo:hi],
+                in_=q_in[a][:, lo:hi].rearrange("p n t -> p (n t)"),
+            )
+
+        def scalar_gather(e):
+            for t in range(4):
+                nc.scalar.activation(
+                    q_in[LAST][:, e * C : (e + 1) * C, t],
+                    planes[:, t].indirect(offs_sb[:, e * C // 16 : (e + 1) * C // 16]),
+                    COPY,
+                )
+
+        def multiply(a, e):
+            for h in range(2):
+                cols = slice(e * C + h * N, e * C + (h + 1) * N)
+                nc.tensor.matmul_mx(
+                    out=banks[2 * e + h][:],
+                    lhsT=w_sb[:, e * PASSES + a, :].bitcast(FP4X4),
+                    lhsT_scale=ws_sb[:, e * PASSES + a, :],
+                    rhs=codes[a][:, cols].bitcast(FP8X4),
+                    rhs_scale=scales[a][:, cols],
+                    start=(a == 0),
+                    stop=(a == LAST),
+                )
+
+        s_in, s_codes, s_scales = {}, {}, {}
+        for a in range(PASSES):
+            s_in[a] = keep.tile([P, T, 4], BF16, name=f"s_in_{a}", align_bytes=64)
+            s_codes[a] = keep.tile([P, T], U32, name=f"s_codes_{a}", align_bytes=64)
+            s_scales[a] = keep.tile([P, T], U8, name=f"s_scales_{a}", align_bytes=64)
+
+        def shared_interleave(a):
+            if a == LAST:
+                nc.scalar.copy(s_in[a][:], raw[a][:].rearrange("p t w -> p w t"))
+            else:
+                nc.vector.tensor_copy(
+                    s_in[a][:].rearrange("p n (u e) -> p n u e", u=2), pairs[a].rearrange("p u w e -> p w u e")
+                )
+
+        def shared_quantize(a):
+            nc.vector.quantize_mx(
+                out=s_codes[a][:].bitcast(FP8X4), scales=s_scales[a][:], in_=s_in[a][:].rearrange("p n t -> p (n t)")
+            )
+
+        cast(0, 0, 0, 320, nc.vector.tensor_copy)
+        cast(0, 0, 320, T, nc.scalar.copy)
+        cast(0, 1, 0, T, nc.scalar.copy)
+        for a in range(1, LAST):
+            for u in range(2):
+                cast(a, u, 0, T, nc.scalar.copy)
+        for u in range(2):
+            nc.scalar.copy(planes[:, 2 * u : 2 * u + 2], raw[LAST][:, 2 * u : 2 * u + 2])
+        for e in range(E):
+            scalar_gather(e)
+        gather(0, 0)
+        gather(0, 1)
+        for a in range(1, LAST):
+            gather(a, 0)
+            interleave(a - 1)
+            gather(a, 1)
+            quantize(a - 1, 0, SLOTS)
+            for e in range(E):
+                multiply(a - 1, e)
+        shared_interleave(0)
+        interleave(LAST - 1)
+        shared_interleave(1)
+        quantize(LAST - 1, 0, SLOTS)
+        for e in range(E):
+            multiply(LAST - 1, e)
+        shared_interleave(2)
+        shared_quantize(0)
+        for e in range(E):
+            if e % 2 == 0:
+                quantize(LAST, e * C, (e + 2) * C)
+            multiply(LAST, e)
+            for h in range(2):
+                nc.scalar.activation(
+                    y_sb[:, e * C + h * N : e * C + (h + 1) * N], banks[2 * e + h][:], RELU, bias=b_sb[:, e : e + 1]
+                )
+        shared_interleave(LAST)
+        shared = psum.tile([P, T], F32, name="shared", tag="bank0")
+        for a in range(PASSES):
+            if a:
+                shared_quantize(a)
+            nc.tensor.matmul_mx(
+                out=shared[:],
+                lhsT=w_sb[:, E * PASSES + a, :].bitcast(FP4X4),
+                lhsT_scale=ws_sb[:, E * PASSES + a, :],
+                rhs=s_codes[a][:].bitcast(FP8X4),
+                rhs_scale=s_scales[a][:],
+                start=(a == 0),
+                stop=(a == LAST),
+            )
+        nc.scalar.activation(ys_sb[:], shared[:], RELU, bias=b_sb[:, E : E + 1])
+
+        half = T // 2
+        first = keep.tile([P, T], F32, name="first")
+        second = keep.tile([P, T], F32, name="second")
+        partial = keep.tile([P, T], F32, name="partial")
+        total = keep.tile([P, T], F32, name="total")
+
+        def pick(dst, r, lst, lo, hi):
+            nc.vector.tensor_tensor(dst[:, lo:hi], y_sb[:].indirect(lst[:, lo // 16 : hi // 16]), gate_sb[:, r, lo:hi], MULT)
+
+        pick(first, 0, pos1_sb, 0, T)
+        pick(second, 1, pos2_sb, 0, half)
+        nc.vector.tensor_add(partial[:], first[:], ys_sb[:])
+        pick(second, 1, pos2_sb, half, T)
+        for h in range(2):
+            cols = slice(h * half, (h + 1) * half)
+            nc.vector.tensor_add(total[:, cols], partial[:, cols], second[:, cols])
+            nc.sync.dma_start(out[:, cols], total[:, cols])

@@ -11,7 +11,6 @@ U8 = mybir.dt.uint8
 FP8X4 = mybir.dt.float8_e4m3fn_x4
 FP4X4 = mybir.dt.float4_e2m1fn_x4
 RELU = mybir.ActivationFunctionType.Relu
-COPY = mybir.ActivationFunctionType.Copy
 MULT = mybir.AluOpType.mult
 
 P = 128
@@ -20,6 +19,7 @@ K_PASS = 512
 PASSES = K // K_PASS
 LAST = PASSES - 1
 SLOTS = E * C
+ROWS = 2 * PASSES
 PIECES = {1: ((0, 384), (384, 768), (768, 1024)), 2: ((0, 768), (768, 1024)), 3: ((0, 1024),)}
 
 FLOPS = 2 * K * N * (SLOTS + T)
@@ -40,31 +40,28 @@ def tile_moe_shr_lin_relu_kernel(tc, xT, w_words, w_scales, b, gate, offs, pos1,
         gate_sb = keep.tile([P, 2, T], F32, name="gate_sb")
         y_sb = keep.tile([P, SLOTS], F32, name="y_sb")
         ys_sb = keep.tile([P, T], F32, name="ys_sb")
-        planes = keep.tile([P, 4, T], BF16, name="planes", align_bytes=64)
         banks = [psum.tile([P, N], F32, name=f"bank{i}", tag=f"bank{i}") for i in range(8)]
-        first_pairs = keep.tile([P, 2, T, 2], BF16, name="first_pairs", align_bytes=64)
-        more_pairs = keep.tile([P, 4, T, 2], BF16, name="more_pairs", align_bytes=64)
-        pairs = {0: first_pairs[:], 1: more_pairs[:, 0:2], 2: more_pairs[:, 2:4]}
-        windows = {(0, 0): first_pairs[:, 0:1], (0, 1): first_pairs[:, 1:2]}
-        for s in range(4):
-            windows[1 + s // 2, s % 2] = more_pairs[:, s : min(s + 3, 4)]
+        pairs = keep.tile([P, ROWS * T * 2], BF16, name="pairs", align_bytes=64)
         raw, gath, q_in, codes, scales = {}, {}, {}, {}, {}
+        s_in, s_scales = {}, {}
         for a in range(PASSES):
-            raw[a] = keep.tile([P, 4, T], F32, name=f"raw_{a}")
+            for u in range(2):
+                raw[a, u] = keep.tile([P, 2, T], F32, name=f"raw_{a}_{u}")
             codes[a] = keep.tile([P, SLOTS], U32, name=f"codes_{a}", align_bytes=64)
             scales[a] = keep.tile([P, SLOTS], U8, name=f"scales_{a}", align_bytes=64)
-            q_in[a] = keep.tile([P, SLOTS, 4], BF16, name=f"q_in_{a}", align_bytes=64)
-            if a != LAST:
-                gath[a] = keep.tile([P, 2, SLOTS, 2], BF16, name=f"gath_{a}", align_bytes=64)
+            q_in[a] = keep.tile([P, SLOTS * 4], BF16, name=f"q_in_{a}", align_bytes=64)
+            gath[a] = keep.tile([P, 2 * SLOTS], U32, name=f"gath_{a}", tag=f"gath_{a}", align_bytes=64)
+            s_in[a] = keep.tile([P, T * 4], BF16, name=f"s_in_{a}", align_bytes=64)
+            s_scales[a] = keep.tile([P, T], U8, name=f"s_scales_{a}", align_bytes=64)
 
         nc.vector.memset(ws_sb[:].rearrange("p g n -> p (g n)").bitcast(I32), 0)
 
-        for a in range(PASSES):
+        order = [(a, u) for a in range(PASSES) for u in (1, 0)]
+        for a, u in order:
             rows = xT[a * K_PASS : (a + 1) * K_PASS, :].rearrange("(p u e) w -> u p e w", u=2, e=2)
-            for u in range(2):
-                nc.sync.dma_start(raw[a][:, 2 * u : 2 * u + 2], rows[u])
-                if a == 0 and u == 0:
-                    nc.sync.dma_start(offs_sb[:], offs)
+            nc.sync.dma_start(raw[a, u][:], rows[u])
+            if (a, u) == order[0]:
+                nc.sync.dma_start(offs_sb[:], offs)
         nc.sync.dma_start(w_sb[:].bitcast(I32), w_words.rearrange("e a p n -> p (e a) n").bitcast(I32))
         scale_rows = w_scales.rearrange("e a q n -> q (e a) n").bitcast(I32)
         for quad in range(4):
@@ -74,36 +71,37 @@ def tile_moe_shr_lin_relu_kernel(tc, xT, w_words, w_scales, b, gate, offs, pos1,
         nc.sync.dma_start(pos2_sb[:], pos2)
         nc.sync.dma_start(gate_sb[:], gate.rearrange("r n t -> n r t"))
 
+        def place(a, u):
+            return 2 * (LAST - a) + u
+
+        def pair_words(first_row, n_rows):
+            return pairs[:, first_row * T * 2 : (first_row + n_rows) * T * 2].bitcast(U32)
+
         def cast(a, u, lo, hi, copy):
-            copy(pairs[a][:, u, lo:hi], raw[a][:, 2 * u : 2 * u + 2, lo:hi].rearrange("p e w -> p w e"))
+            base = place(a, u) * T * 2
+            copy(
+                pairs[:, base + 2 * lo : base + 2 * hi].rearrange("p (w e) -> p w e", e=2),
+                raw[a, u][:, :, lo:hi].rearrange("p e w -> p w e"),
+            )
 
         def gather(a, u):
-            window = windows[a, u]
-            for lo, hi in PIECES[window.shape[1]]:
+            n_rows = min(3, ROWS - place(a, u))
+            for lo, hi in PIECES[n_rows]:
                 nc.vector.tensor_copy(
-                    gath[a][:, u, lo:hi].rearrange("p n e -> p (n e)").bitcast(U32),
-                    window.rearrange("p s w e -> p (s w e)").bitcast(U32).indirect(offs_sb[:, lo // 16 : hi // 16]),
+                    gath[a][:, u * SLOTS + lo : u * SLOTS + hi],
+                    pair_words(place(a, u), n_rows).indirect(offs_sb[:, lo // 16 : hi // 16]),
                 )
 
         def interleave(a):
-            nc.vector.tensor_copy(
-                q_in[a][:].rearrange("p n (u e) -> p n u e", u=2), gath[a][:].rearrange("p u n e -> p n u e")
+            nc.scalar.copy(
+                q_in[a][:].bitcast(U32).rearrange("p (n u) -> p n u", u=2),
+                gath[a][:].rearrange("p (u n) -> p n u", u=2),
             )
 
         def quantize(a, lo, hi):
             nc.vector.quantize_mx(
-                out=codes[a][:, lo:hi].bitcast(FP8X4),
-                scales=scales[a][:, lo:hi],
-                in_=q_in[a][:, lo:hi].rearrange("p n t -> p (n t)"),
+                out=codes[a][:, lo:hi].bitcast(FP8X4), scales=scales[a][:, lo:hi], in_=q_in[a][:, 4 * lo : 4 * hi]
             )
-
-        def scalar_gather(e):
-            for t in range(4):
-                nc.scalar.activation(
-                    q_in[LAST][:, e * C : (e + 1) * C, t],
-                    planes[:, t].indirect(offs_sb[:, e * C // 16 : (e + 1) * C // 16]),
-                    COPY,
-                )
 
         def multiply(a, e):
             for h in range(2):
@@ -118,52 +116,31 @@ def tile_moe_shr_lin_relu_kernel(tc, xT, w_words, w_scales, b, gate, offs, pos1,
                     stop=(a == LAST),
                 )
 
-        s_in, s_codes, s_scales = {}, {}, {}
-        for a in range(PASSES):
-            s_in[a] = keep.tile([P, T, 4], BF16, name=f"s_in_{a}", align_bytes=64)
-            s_codes[a] = keep.tile([P, T], U32, name=f"s_codes_{a}", align_bytes=64)
-            s_scales[a] = keep.tile([P, T], U8, name=f"s_scales_{a}", align_bytes=64)
-
         def shared_interleave(a):
-            if a == LAST:
-                nc.scalar.copy(s_in[a][:], raw[a][:].rearrange("p t w -> p w t"))
-            else:
-                nc.vector.tensor_copy(
-                    s_in[a][:].rearrange("p n (u e) -> p n u e", u=2), pairs[a].rearrange("p u w e -> p w u e")
-                )
-
-        def shared_quantize(a):
-            nc.vector.quantize_mx(
-                out=s_codes[a][:].bitcast(FP8X4), scales=s_scales[a][:], in_=s_in[a][:].rearrange("p n t -> p (n t)")
+            nc.scalar.copy(
+                s_in[a][:].bitcast(U32).rearrange("p (w u) -> p w u", u=2),
+                pair_words(place(a, 0), 2).rearrange("p (u w) -> p w u", u=2),
             )
 
-        cast(0, 0, 0, 320, nc.vector.tensor_copy)
-        cast(0, 0, 320, T, nc.scalar.copy)
-        cast(0, 1, 0, T, nc.scalar.copy)
-        for a in range(1, LAST):
-            for u in range(2):
+        def shared_quantize(a):
+            nc.vector.quantize_mx(out=s_codes[:, a * T : (a + 1) * T].bitcast(FP8X4), scales=s_scales[a][:], in_=s_in[a][:])
+
+        for a, u in order:
+            if (a, u) == order[0]:
+                cast(a, u, 0, 320, nc.vector.tensor_copy)
+                cast(a, u, 320, T, nc.scalar.copy)
+            else:
                 cast(a, u, 0, T, nc.scalar.copy)
-        for u in range(2):
-            nc.scalar.copy(planes[:, 2 * u : 2 * u + 2], raw[LAST][:, 2 * u : 2 * u + 2])
-        for e in range(E):
-            scalar_gather(e)
-        gather(0, 0)
-        gather(0, 1)
-        for a in range(1, LAST):
-            gather(a, 0)
-            interleave(a - 1)
-            gather(a, 1)
-            quantize(a - 1, 0, SLOTS)
-            for e in range(E):
-                multiply(a - 1, e)
-        shared_interleave(0)
-        interleave(LAST - 1)
-        shared_interleave(1)
-        quantize(LAST - 1, 0, SLOTS)
-        for e in range(E):
-            multiply(LAST - 1, e)
-        shared_interleave(2)
-        shared_quantize(0)
+            gather(a, u)
+        for a in range(PASSES):
+            shared_interleave(a)
+        for a in range(PASSES):
+            interleave(a)
+            if a != LAST:
+                quantize(a, 0, SLOTS)
+                for e in range(E):
+                    multiply(a, e)
+        s_codes = keep.tile([P, PASSES * T], U32, name="s_codes", tag=f"gath_{LAST}", align_bytes=64)
         for e in range(E):
             if e % 2 == 0:
                 quantize(LAST, e * C, (e + 2) * C)
@@ -172,16 +149,14 @@ def tile_moe_shr_lin_relu_kernel(tc, xT, w_words, w_scales, b, gate, offs, pos1,
                 nc.scalar.activation(
                     y_sb[:, e * C + h * N : e * C + (h + 1) * N], banks[2 * e + h][:], RELU, bias=b_sb[:, e : e + 1]
                 )
-        shared_interleave(LAST)
         shared = psum.tile([P, T], F32, name="shared", tag="bank0")
         for a in range(PASSES):
-            if a:
-                shared_quantize(a)
+            shared_quantize(a)
             nc.tensor.matmul_mx(
                 out=shared[:],
                 lhsT=w_sb[:, E * PASSES + a, :].bitcast(FP4X4),
                 lhsT_scale=ws_sb[:, E * PASSES + a, :],
-                rhs=s_codes[a][:].bitcast(FP8X4),
+                rhs=s_codes[:, a * T : (a + 1) * T].bitcast(FP8X4),
                 rhs_scale=s_scales[a][:],
                 start=(a == 0),
                 stop=(a == LAST),

@@ -117,7 +117,8 @@ def tile_moe_shr_lin_relu_kernel(tc, xT, w_words, w_scales, b, gate, offs, pos1,
                 )
 
         def shared_interleave(a):
-            nc.scalar.copy(
+            copy = nc.gpsimd.tensor_copy if a < 2 else nc.scalar.copy
+            copy(
                 s_in[a][:].bitcast(U32).rearrange("p (w u) -> p w u", u=2),
                 pair_words(place(a, 0), 2).rearrange("p (u w) -> p w u", u=2),
             )

@@ -11,6 +11,7 @@ U8 = mybir.dt.uint8
 FP8X4 = mybir.dt.float8_e4m3fn_x4
 FP4X4 = mybir.dt.float4_e2m1fn_x4
 RELU = mybir.ActivationFunctionType.Relu
+COPY = mybir.ActivationFunctionType.Copy
 MULT = mybir.AluOpType.mult
 
 P = 128
@@ -20,6 +21,7 @@ PASSES = K // K_PASS
 LAST = PASSES - 1
 SLOTS = E * C
 ROWS = 2 * PASSES
+ORDER = ((0, 1), (0, 0), (LAST, 1), (1, 1), (1, 0), (LAST, 0), (2, 1), (2, 0))
 PIECES = {1: ((0, 384), (384, 768), (768, 1024)), 2: ((0, 768), (768, 1024)), 3: ((0, 1024),)}
 
 FLOPS = 2 * K * N * (SLOTS + T)
@@ -44,23 +46,28 @@ def tile_moe_shr_lin_relu_kernel(tc, xT, w_words, w_scales, b, gate, offs, pos1,
         pairs = keep.tile([P, ROWS * T * 2], BF16, name="pairs", align_bytes=64)
         raw, gath, q_in, codes, scales = {}, {}, {}, {}, {}
         s_in, s_scales = {}, {}
+        raw_last = keep.tile([P, 4, T], F32, name="raw_last")
         for a in range(PASSES):
             for u in range(2):
-                raw[a, u] = keep.tile([P, 2, T], F32, name=f"raw_{a}_{u}")
-            codes[a] = keep.tile([P, SLOTS], U32, name=f"codes_{a}", align_bytes=64)
+                if a == LAST:
+                    raw[a, u] = raw_last[:, 2 * u : 2 * u + 2]
+                else:
+                    raw[a, u] = keep.tile([P, 2, T], F32, name=f"raw_{a}_{u}", tag=f"raw_{a}_{u}", align_bytes=64)[:]
             scales[a] = keep.tile([P, SLOTS], U8, name=f"scales_{a}", align_bytes=64)
-            q_in[a] = keep.tile([P, SLOTS * 4], BF16, name=f"q_in_{a}", align_bytes=64)
-            gath[a] = keep.tile([P, 2 * SLOTS], U32, name=f"gath_{a}", tag=f"gath_{a}", align_bytes=64)
-            s_in[a] = keep.tile([P, T * 4], BF16, name=f"s_in_{a}", align_bytes=64)
             s_scales[a] = keep.tile([P, T], U8, name=f"s_scales_{a}", align_bytes=64)
+            if a != LAST:
+                codes[a] = keep.tile([P, SLOTS], U32, name=f"codes_{a}", align_bytes=64)
+                gath[a] = keep.tile([P, 2 * SLOTS], U32, name=f"gath_{a}", tag=f"gath_{a}", align_bytes=64)
+                s_in[a] = keep.tile([P, T * 4], BF16, name=f"s_in_{a}", align_bytes=64)
+        for a in (LAST - 1, LAST):
+            q_in[a] = keep.tile([P, SLOTS * 4], BF16, name=f"q_in_{a}", tag=f"q_in_{a}", align_bytes=64)[:]
 
         nc.vector.memset(ws_sb[:].rearrange("p g n -> p (g n)").bitcast(I32), 0)
 
-        order = [(a, u) for a in range(PASSES) for u in (1, 0)]
-        for a, u in order:
+        for a, u in ORDER:
             rows = xT[a * K_PASS : (a + 1) * K_PASS, :].rearrange("(p u e) w -> u p e w", u=2, e=2)
-            nc.sync.dma_start(raw[a, u][:], rows[u])
-            if (a, u) == order[0]:
+            nc.sync.dma_start(raw[a, u], rows[u])
+            if (a, u) == ORDER[0]:
                 nc.sync.dma_start(offs_sb[:], offs)
         nc.sync.dma_start(w_sb[:].bitcast(I32), w_words.rearrange("e a p n -> p (e a) n").bitcast(I32))
         scale_rows = w_scales.rearrange("e a q n -> q (e a) n").bitcast(I32)
@@ -72,7 +79,7 @@ def tile_moe_shr_lin_relu_kernel(tc, xT, w_words, w_scales, b, gate, offs, pos1,
         nc.sync.dma_start(gate_sb[:], gate.rearrange("r n t -> n r t"))
 
         def place(a, u):
-            return 2 * (LAST - a) + u
+            return ROWS - 1 - ORDER.index((a, u))
 
         def pair_words(first_row, n_rows):
             return pairs[:, first_row * T * 2 : (first_row + n_rows) * T * 2].bitcast(U32)
@@ -92,10 +99,29 @@ def tile_moe_shr_lin_relu_kernel(tc, xT, w_words, w_scales, b, gate, offs, pos1,
                     pair_words(place(a, u), n_rows).indirect(offs_sb[:, lo // 16 : hi // 16]),
                 )
 
-        def interleave(a):
-            nc.scalar.copy(
-                q_in[a][:].bitcast(U32).rearrange("p (n u) -> p n u", u=2),
-                gath[a][:].rearrange("p (u n) -> p n u", u=2),
+        def cast_planes(u, copy):
+            base = place(LAST, u) * T * 2
+            copy(pairs[:, base : base + 2 * T], raw[LAST, u].rearrange("p e w -> p (e w)"))
+
+        def scalar_gather(u):
+            for e in range(2):
+                base = place(LAST, u) * T * 2 + e * T
+                nc.scalar.activation(
+                    q_in[LAST].rearrange("p (n t) -> p n t", t=4)[:, :, 2 * u + e],
+                    pairs[:, base : base + 3 * T].indirect(offs_sb[:]),
+                    COPY,
+                )
+
+        def interleave(a, lo, hi, copy):
+            copy(
+                q_in[a].bitcast(U32).rearrange("p (n u) -> p n u", u=2)[:, lo:hi],
+                gath[a][:].rearrange("p (u n) -> p n u", u=2)[:, lo:hi],
+            )
+
+        def vector_interleave(a, lo, hi):
+            nc.vector.tensor_copy(
+                q_in[a].rearrange("p (n u e) -> p n u e", u=2, e=2)[:, lo:hi],
+                gath[a][:].bitcast(BF16).rearrange("p (u n e) -> p n u e", u=2, e=2)[:, lo:hi],
             )
 
         def quantize(a, lo, hi):
@@ -117,8 +143,7 @@ def tile_moe_shr_lin_relu_kernel(tc, xT, w_words, w_scales, b, gate, offs, pos1,
                 )
 
         def shared_interleave(a):
-            copy = nc.gpsimd.tensor_copy if a < 2 else nc.scalar.copy
-            copy(
+            nc.scalar.copy(
                 s_in[a][:].bitcast(U32).rearrange("p (w u) -> p w u", u=2),
                 pair_words(place(a, 0), 2).rearrange("p (u w) -> p w u", u=2),
             )
@@ -126,33 +151,7 @@ def tile_moe_shr_lin_relu_kernel(tc, xT, w_words, w_scales, b, gate, offs, pos1,
         def shared_quantize(a):
             nc.vector.quantize_mx(out=s_codes[:, a * T : (a + 1) * T].bitcast(FP8X4), scales=s_scales[a][:], in_=s_in[a][:])
 
-        for a, u in order:
-            if (a, u) == order[0]:
-                cast(a, u, 0, 320, nc.vector.tensor_copy)
-                cast(a, u, 320, T, nc.scalar.copy)
-            else:
-                cast(a, u, 0, T, nc.scalar.copy)
-            gather(a, u)
-        for a in range(PASSES):
-            shared_interleave(a)
-        for a in range(PASSES):
-            interleave(a)
-            if a != LAST:
-                quantize(a, 0, SLOTS)
-                for e in range(E):
-                    multiply(a, e)
-        s_codes = keep.tile([P, PASSES * T], U32, name="s_codes", tag=f"gath_{LAST}", align_bytes=64)
-        for e in range(E):
-            if e % 2 == 0:
-                quantize(LAST, e * C, (e + 2) * C)
-            multiply(LAST, e)
-            for h in range(2):
-                nc.scalar.activation(
-                    y_sb[:, e * C + h * N : e * C + (h + 1) * N], banks[2 * e + h][:], RELU, bias=b_sb[:, e : e + 1]
-                )
-        shared = psum.tile([P, T], F32, name="shared", tag="bank0")
-        for a in range(PASSES):
-            shared_quantize(a)
+        def shared_multiply(a):
             nc.tensor.matmul_mx(
                 out=shared[:],
                 lhsT=w_sb[:, E * PASSES + a, :].bitcast(FP4X4),
@@ -162,6 +161,47 @@ def tile_moe_shr_lin_relu_kernel(tc, xT, w_words, w_scales, b, gate, offs, pos1,
                 start=(a == 0),
                 stop=(a == LAST),
             )
+
+        for step, (a, u) in enumerate(ORDER):
+            copy = nc.scalar.copy if step < 3 else nc.gpsimd.tensor_copy
+            if a == LAST:
+                cast_planes(u, copy)
+                scalar_gather(u)
+            else:
+                if step == 0:
+                    cast(a, u, 0, 320, nc.vector.tensor_copy)
+                    cast(a, u, 320, T, copy)
+                else:
+                    cast(a, u, 0, T, copy)
+                gather(a, u)
+        q_early = keep.tile([P, 2 * SLOTS * 4], BF16, name="q_early", tag="raw_2_0", align_bytes=64)
+        for a in range(2):
+            q_in[a] = q_early[:, a * SLOTS * 4 : (a + 1) * SLOTS * 4]
+        interleave(0, 0, SLOTS, nc.gpsimd.tensor_copy)
+        interleave(1, 0, SLOTS // 2, nc.gpsimd.tensor_copy)
+        vector_interleave(1, SLOTS // 2, SLOTS)
+        vector_interleave(2, 0, SLOTS)
+        for a in range(LAST):
+            shared_interleave(a)
+            quantize(a, 0, SLOTS)
+            for e in range(E):
+                multiply(a, e)
+        s_in[LAST] = keep.tile([P, T * 4], BF16, name="s_in_last", align_bytes=64)
+        nc.scalar.copy(s_in[LAST][:].rearrange("p (w t) -> p w t", t=4), raw_last[:].rearrange("p t w -> p w t"))
+        codes[LAST] = keep.tile([P, SLOTS], U32, name="codes_last", tag=f"gath_{LAST - 1}", align_bytes=64)
+        for e in range(E):
+            if e % 2 == 0:
+                quantize(LAST, e * C, (e + 2) * C)
+            multiply(LAST, e)
+            for h in range(2):
+                nc.scalar.activation(
+                    y_sb[:, e * C + h * N : e * C + (h + 1) * N], banks[2 * e + h][:], RELU, bias=b_sb[:, e : e + 1]
+                )
+        s_codes = keep.tile([P, PASSES * T], U32, name="s_codes", tag=f"q_in_{LAST}", align_bytes=64)
+        shared = psum.tile([P, T], F32, name="shared", tag="bank0")
+        for a in range(PASSES):
+            shared_quantize(a)
+            shared_multiply(a)
         nc.scalar.activation(ys_sb[:], shared[:], RELU, bias=b_sb[:, E : E + 1])
 
         half = T // 2

@@ -20,8 +20,9 @@ K_PASS = 512
 PASSES = K // K_PASS
 LAST = PASSES - 1
 SLOTS = E * C
-ROWS = 2 * PASSES
-ORDER = ((0, 1), (0, 0), (LAST, 1), (1, 1), (1, 0), (LAST, 0), (2, 1), (2, 0))
+ROWS = 4 * PASSES
+ORDER = ((0, 2, 2), (LAST, 3, 1), (0, 0, 2), (LAST, 2, 1), (1, 2, 2), (1, 0, 2), (LAST, 0, 2), (2, 2, 2), (2, 0, 2))
+SUM_ORDER = (0, 1, LAST, 2)
 PIECES = {1: ((0, 384), (384, 768), (768, 1024)), 2: ((0, 768), (768, 1024)), 3: ((0, 1024),)}
 
 FLOPS = 2 * K * N * (SLOTS + T)
@@ -43,31 +44,39 @@ def tile_moe_shr_lin_relu_kernel(tc, xT, w_words, w_scales, b, gate, offs, pos1,
         y_sb = keep.tile([P, SLOTS], F32, name="y_sb")
         ys_sb = keep.tile([P, T], F32, name="ys_sb")
         banks = [psum.tile([P, N], F32, name=f"bank{i}", tag=f"bank{i}") for i in range(8)]
-        pairs = keep.tile([P, ROWS * T * 2], BF16, name="pairs", align_bytes=64)
+        cast_sb = keep.tile([P, (ROWS + 1) * T], BF16, name="cast_sb", align_bytes=64)
         raw, gath, q_in, codes, scales = {}, {}, {}, {}, {}
         s_in, s_scales = {}, {}
         raw_last = keep.tile([P, 4, T], F32, name="raw_last")
+        place, top = {}, ROWS
+        for a, t, n_rows in ORDER:
+            top -= n_rows
+            place[a, t] = top
+            if a == LAST:
+                raw[a, t] = raw_last[:, t : t + n_rows]
+            else:
+                raw[a, t] = keep.tile([P, 2, T], F32, name=f"raw_{a}_{t}", tag=f"raw_{a}_{t}", align_bytes=64)[:]
         for a in range(PASSES):
-            for u in range(2):
-                if a == LAST:
-                    raw[a, u] = raw_last[:, 2 * u : 2 * u + 2]
-                else:
-                    raw[a, u] = keep.tile([P, 2, T], F32, name=f"raw_{a}_{u}", tag=f"raw_{a}_{u}", align_bytes=64)[:]
             scales[a] = keep.tile([P, SLOTS], U8, name=f"scales_{a}", align_bytes=64)
             s_scales[a] = keep.tile([P, T], U8, name=f"s_scales_{a}", align_bytes=64)
             if a != LAST:
-                codes[a] = keep.tile([P, SLOTS], U32, name=f"codes_{a}", align_bytes=64)
+                codes[a] = keep.tile([P, SLOTS], U32, name=f"codes_{a}", tag=f"codes_{a}", align_bytes=64)
                 gath[a] = keep.tile([P, 2 * SLOTS], U32, name=f"gath_{a}", tag=f"gath_{a}", align_bytes=64)
-                s_in[a] = keep.tile([P, T * 4], BF16, name=f"s_in_{a}", align_bytes=64)
-        for a in (LAST - 1, LAST):
+        for a in (2, LAST):
             q_in[a] = keep.tile([P, SLOTS * 4], BF16, name=f"q_in_{a}", tag=f"q_in_{a}", align_bytes=64)[:]
 
+        half = T // 2
+        halves = (slice(0, half), slice(half, T))
         nc.vector.memset(ws_sb[:].rearrange("p g n -> p (g n)").bitcast(I32), 0)
 
-        for a, u in ORDER:
-            rows = xT[a * K_PASS : (a + 1) * K_PASS, :].rearrange("(p u e) w -> u p e w", u=2, e=2)
-            nc.sync.dma_start(raw[a, u], rows[u])
-            if (a, u) == ORDER[0]:
+        for step, (a, t, n_rows) in enumerate(ORDER):
+            rows = xT[a * K_PASS : (a + 1) * K_PASS, :].rearrange("(p t) w -> p t w", t=4)
+            if a == 0:
+                for cols in halves:
+                    nc.sync.dma_start(raw[a, t][:, :, cols], rows[:, t : t + n_rows, cols])
+            else:
+                nc.sync.dma_start(raw[a, t], rows[:, t : t + n_rows])
+            if step == 0:
                 nc.sync.dma_start(offs_sb[:], offs)
         nc.sync.dma_start(w_sb[:].bitcast(I32), w_words.rearrange("e a p n -> p (e a) n").bitcast(I32))
         scale_rows = w_scales.rearrange("e a q n -> q (e a) n").bitcast(I32)
@@ -78,37 +87,32 @@ def tile_moe_shr_lin_relu_kernel(tc, xT, w_words, w_scales, b, gate, offs, pos1,
         nc.sync.dma_start(pos2_sb[:], pos2)
         nc.sync.dma_start(gate_sb[:], gate.rearrange("r n t -> n r t"))
 
-        def place(a, u):
-            return ROWS - 1 - ORDER.index((a, u))
-
-        def pair_words(first_row, n_rows):
-            return pairs[:, first_row * T * 2 : (first_row + n_rows) * T * 2].bitcast(U32)
-
-        def cast(a, u, lo, hi, copy):
-            base = place(a, u) * T * 2
+        def cast_pairs(a, t, lo, hi, copy):
+            base = place[a, t] * T
             copy(
-                pairs[:, base + 2 * lo : base + 2 * hi].rearrange("p (w e) -> p w e", e=2),
-                raw[a, u][:, :, lo:hi].rearrange("p e w -> p w e"),
+                cast_sb[:, base + 2 * lo : base + 2 * hi].rearrange("p (w e) -> p w e", e=2),
+                raw[a, t][:, :, lo:hi].rearrange("p e w -> p w e"),
             )
 
-        def gather(a, u):
-            n_rows = min(3, ROWS - place(a, u))
-            for lo, hi in PIECES[n_rows]:
+        def gather_pairs(a, t):
+            n_pairs = min(3, (ROWS - place[a, t]) // 2)
+            window = cast_sb[:, place[a, t] * T : (place[a, t] + 2 * n_pairs) * T].bitcast(U32)
+            for lo, hi in PIECES[n_pairs]:
                 nc.vector.tensor_copy(
-                    gath[a][:, u * SLOTS + lo : u * SLOTS + hi],
-                    pair_words(place(a, u), n_rows).indirect(offs_sb[:, lo // 16 : hi // 16]),
+                    gath[a][:, t // 2 * SLOTS + lo : t // 2 * SLOTS + hi],
+                    window.indirect(offs_sb[:, lo // 16 : hi // 16]),
                 )
 
-        def cast_planes(u, copy):
-            base = place(LAST, u) * T * 2
-            copy(pairs[:, base : base + 2 * T], raw[LAST, u].rearrange("p e w -> p (e w)"))
+        def cast_rows(t, n_rows, copy):
+            base = place[LAST, t] * T
+            copy(cast_sb[:, base : base + n_rows * T], raw[LAST, t].rearrange("p e w -> p (e w)"))
 
-        def scalar_gather(u):
-            for e in range(2):
-                base = place(LAST, u) * T * 2 + e * T
+        def gather_rows(t, n_rows):
+            for e in range(n_rows):
+                base = (place[LAST, t] + e) * T
                 nc.scalar.activation(
-                    q_in[LAST].rearrange("p (n t) -> p n t", t=4)[:, :, 2 * u + e],
-                    pairs[:, base : base + 3 * T].indirect(offs_sb[:]),
+                    q_in[LAST].rearrange("p (n t) -> p n t", t=4)[:, :, t + e],
+                    cast_sb[:, base : base + 3 * T].indirect(offs_sb[:]),
                     COPY,
                 )
 
@@ -138,18 +142,28 @@ def tile_moe_shr_lin_relu_kernel(tc, xT, w_words, w_scales, b, gate, offs, pos1,
                     lhsT_scale=ws_sb[:, e * PASSES + a, :],
                     rhs=codes[a][:, cols].bitcast(FP8X4),
                     rhs_scale=scales[a][:, cols],
-                    start=(a == 0),
-                    stop=(a == LAST),
+                    start=(a == SUM_ORDER[0]),
+                    stop=(a == SUM_ORDER[-1]),
                 )
 
         def shared_interleave(a):
+            base, pitch = place[a, 0] * T, (place[a, 2] - place[a, 0]) * T
+            words = cast_sb[:, base : base + 2 * pitch].bitcast(U32).rearrange("p (u w) -> p w u", u=2)
+            nc.scalar.copy(s_in[a].bitcast(U32).rearrange("p (w u) -> p w u", u=2), words[:, 0:T])
+
+        def shared_rows(dst, lo, hi):
             nc.scalar.copy(
-                s_in[a][:].bitcast(U32).rearrange("p (w u) -> p w u", u=2),
-                pair_words(place(a, 0), 2).rearrange("p (u w) -> p w u", u=2),
+                dst.rearrange("p (c i t) -> p c t i", i=4, t=4),
+                raw_last[:, :, lo:hi].rearrange("p t (c i) -> p c t i", i=4),
+            )
+
+        def shared_quantize_last(src, lo, hi):
+            nc.vector.quantize_mx(
+                out=s_codes[:, LAST * T + lo : LAST * T + hi].bitcast(FP8X4), scales=s_scales[LAST][:, lo:hi], in_=src
             )
 
         def shared_quantize(a):
-            nc.vector.quantize_mx(out=s_codes[:, a * T : (a + 1) * T].bitcast(FP8X4), scales=s_scales[a][:], in_=s_in[a][:])
+            nc.vector.quantize_mx(out=s_codes[:, a * T : (a + 1) * T].bitcast(FP8X4), scales=s_scales[a][:], in_=s_in[a])
 
         def shared_multiply(a):
             nc.tensor.matmul_mx(
@@ -162,62 +176,72 @@ def tile_moe_shr_lin_relu_kernel(tc, xT, w_words, w_scales, b, gate, offs, pos1,
                 stop=(a == LAST),
             )
 
-        for step, (a, u) in enumerate(ORDER):
-            copy = nc.scalar.copy if step < 3 else nc.gpsimd.tensor_copy
+        for step, (a, t, n_rows) in enumerate(ORDER):
+            copy = nc.scalar.copy if step < 2 else nc.gpsimd.tensor_copy
             if a == LAST:
-                cast_planes(u, copy)
-                scalar_gather(u)
+                cast_rows(t, n_rows, copy)
+                gather_rows(t, n_rows)
             else:
                 if step == 0:
-                    cast(a, u, 0, 320, nc.vector.tensor_copy)
-                    cast(a, u, 320, T, copy)
+                    cast_pairs(a, t, 0, half, nc.vector.tensor_copy)
+                    cast_pairs(a, t, half, 416, nc.vector.tensor_copy)
+                    cast_pairs(a, t, 416, T, copy)
+                elif a == 0:
+                    cast_pairs(a, t, 0, half, copy)
+                    cast_pairs(a, t, half, T, copy)
                 else:
-                    cast(a, u, 0, T, copy)
-                gather(a, u)
+                    cast_pairs(a, t, 0, T, copy)
+                gather_pairs(a, t)
         q_early = keep.tile([P, 2 * SLOTS * 4], BF16, name="q_early", tag="raw_2_0", align_bytes=64)
+        s_early = keep.tile([P, (LAST * T + half) * 4], BF16, name="s_early", tag="raw_2_2", align_bytes=64)
         for a in range(2):
             q_in[a] = q_early[:, a * SLOTS * 4 : (a + 1) * SLOTS * 4]
+        for a in range(LAST):
+            s_in[a] = s_early[:, a * T * 4 : (a + 1) * T * 4]
         interleave(0, 0, SLOTS, nc.gpsimd.tensor_copy)
         interleave(1, 0, SLOTS // 2, nc.gpsimd.tensor_copy)
         vector_interleave(1, SLOTS // 2, SLOTS)
-        vector_interleave(2, 0, SLOTS)
-        for a in range(LAST):
-            shared_interleave(a)
+        shared_interleave(0)
+        interleave(2, 0, SLOTS, nc.scalar.copy)
+        shared_interleave(1)
+        shared_interleave(2)
+        shared_rows(s_early[:, LAST * T * 4 :], 0, half)
+        codes[LAST] = keep.tile([P, SLOTS], U32, name="codes_last", tag="gath_1", align_bytes=64)
+        for a in SUM_ORDER[:-1]:
             quantize(a, 0, SLOTS)
             for e in range(E):
                 multiply(a, e)
-        s_in[LAST] = keep.tile([P, T * 4], BF16, name="s_in_last", align_bytes=64)
-        nc.scalar.copy(s_in[LAST][:].rearrange("p (w t) -> p w t", t=4), raw_last[:].rearrange("p t w -> p w t"))
-        codes[LAST] = keep.tile([P, SLOTS], U32, name="codes_last", tag=f"gath_{LAST - 1}", align_bytes=64)
         for e in range(E):
             if e % 2 == 0:
-                quantize(LAST, e * C, (e + 2) * C)
-            multiply(LAST, e)
+                quantize(SUM_ORDER[-1], e * C, (e + 2) * C)
+            multiply(SUM_ORDER[-1], e)
             for h in range(2):
                 nc.scalar.activation(
                     y_sb[:, e * C + h * N : e * C + (h + 1) * N], banks[2 * e + h][:], RELU, bias=b_sb[:, e : e + 1]
                 )
-        s_codes = keep.tile([P, PASSES * T], U32, name="s_codes", tag=f"q_in_{LAST}", align_bytes=64)
+        s_codes = keep.tile([P, PASSES * T], U32, name="s_codes", tag="q_in_2", align_bytes=64)
+        s_late = keep.tile([P, half * 4], BF16, name="s_late", tag="codes_2", align_bytes=64)
+        shared_rows(s_late[:], half, T)
         shared = psum.tile([P, T], F32, name="shared", tag="bank0")
-        for a in range(PASSES):
+        for a in range(LAST):
             shared_quantize(a)
             shared_multiply(a)
-        nc.scalar.activation(ys_sb[:], shared[:], RELU, bias=b_sb[:, E : E + 1])
+        shared_quantize_last(s_early[:, LAST * T * 4 :], 0, half)
 
-        half = T // 2
         first = keep.tile([P, T], F32, name="first")
-        second = keep.tile([P, T], F32, name="second")
         partial = keep.tile([P, T], F32, name="partial")
         total = keep.tile([P, T], F32, name="total")
 
         def pick(dst, r, lst, lo, hi):
-            nc.vector.tensor_tensor(dst[:, lo:hi], y_sb[:].indirect(lst[:, lo // 16 : hi // 16]), gate_sb[:, r, lo:hi], MULT)
+            nc.vector.tensor_tensor(dst, y_sb[:].indirect(lst[:, lo // 16 : hi // 16]), gate_sb[:, r, lo:hi], MULT)
 
-        pick(first, 0, pos1_sb, 0, T)
-        pick(second, 1, pos2_sb, 0, half)
+        pick(first[:], 0, pos1_sb, 0, T)
+        shared_quantize_last(s_late[:], half, T)
+        shared_multiply(LAST)
+        nc.scalar.activation(ys_sb[:], shared[:], RELU, bias=b_sb[:, E : E + 1])
+        second = keep.tile([P, T], F32, name="second", tag="codes_2", align_bytes=64)
+        pick(second[:], 1, pos2_sb, 0, T)
         nc.vector.tensor_add(partial[:], first[:], ys_sb[:])
-        pick(second, 1, pos2_sb, half, T)
-        for h in range(2):
-            cols = slice(h * half, (h + 1) * half)
+        for cols in halves:
             nc.vector.tensor_add(total[:, cols], partial[:, cols], second[:, cols])
             nc.sync.dma_start(out[:, cols], total[:, cols])

@@ -61,7 +61,7 @@ def tile_moe_shr_lin_relu_kernel(tc, xT, w_words, w_scales, b, gate, offs, pos1,
             s_scales[a] = keep.tile([P, T], U8, name=f"s_scales_{a}", align_bytes=64)
             if a != LAST:
                 codes[a] = keep.tile([P, SLOTS], U32, name=f"codes_{a}", tag=f"codes_{a}", align_bytes=64)
-                gath[a] = keep.tile([P, 2 * SLOTS], U32, name=f"gath_{a}", tag=f"gath_{a}", align_bytes=64)
+            gath[a] = keep.tile([P, 2 * SLOTS], U32, name=f"gath_{a}", tag=f"gath_{a}", align_bytes=64)
         for a in (2, LAST):
             q_in[a] = keep.tile([P, SLOTS * 4], BF16, name=f"q_in_{a}", tag=f"q_in_{a}", align_bytes=64)[:]
 
@@ -111,7 +111,7 @@ def tile_moe_shr_lin_relu_kernel(tc, xT, w_words, w_scales, b, gate, offs, pos1,
             for e in range(n_rows):
                 base = (place[LAST, t] + e) * T
                 nc.scalar.activation(
-                    q_in[LAST].rearrange("p (n t) -> p n t", t=4)[:, :, t + e],
+                    gath[LAST][:].bitcast(BF16).rearrange("p (u n e) -> p u n e", u=2, e=2)[:, (t + e) // 2, :, (t + e) % 2],
                     cast_sb[:, base : base + 3 * T].indirect(offs_sb[:]),
                     COPY,
                 )
@@ -201,6 +201,7 @@ def tile_moe_shr_lin_relu_kernel(tc, xT, w_words, w_scales, b, gate, offs, pos1,
         interleave(0, 0, SLOTS, nc.gpsimd.tensor_copy)
         interleave(1, 0, SLOTS // 2, nc.gpsimd.tensor_copy)
         vector_interleave(1, SLOTS // 2, SLOTS)
+        interleave(LAST, 0, SLOTS, nc.scalar.copy)
         shared_interleave(0)
         interleave(2, 0, SLOTS, nc.scalar.copy)
         shared_interleave(1)

@@ -47,7 +47,7 @@ def tile_moe_shr_lin_relu_kernel(tc, xT, w_words, w_scales, b, gate, offs, pos1,
         cast_sb = keep.tile([P, (ROWS + 1) * T], BF16, name="cast_sb", align_bytes=64)
         raw, gath, q_in, codes, scales = {}, {}, {}, {}, {}
         s_in, s_scales = {}, {}
-        raw_last = keep.tile([P, 4, T], F32, name="raw_last")
+        raw_last = keep.tile([P, 4, T], F32, name="raw_last", tag="raw_last")
         place, top = {}, ROWS
         for a, t, n_rows in ORDER:
             top -= n_rows
@@ -59,11 +59,11 @@ def tile_moe_shr_lin_relu_kernel(tc, xT, w_words, w_scales, b, gate, offs, pos1,
         for a in range(PASSES):
             scales[a] = keep.tile([P, SLOTS], U8, name=f"scales_{a}", align_bytes=64)
             s_scales[a] = keep.tile([P, T], U8, name=f"s_scales_{a}", align_bytes=64)
-            if a != LAST:
-                codes[a] = keep.tile([P, SLOTS], U32, name=f"codes_{a}", tag=f"codes_{a}", align_bytes=64)
+            if a < 2:
+                codes[a] = keep.tile([P, SLOTS], U32, name=f"codes_{a}", align_bytes=64)
             gath[a] = keep.tile([P, 2 * SLOTS], U32, name=f"gath_{a}", tag=f"gath_{a}", align_bytes=64)
-        for a in (2, LAST):
-            q_in[a] = keep.tile([P, SLOTS * 4], BF16, name=f"q_in_{a}", tag=f"q_in_{a}", align_bytes=64)[:]
+        q_in[LAST] = keep.tile([P, SLOTS * 4], BF16, name="q_in_last", align_bytes=64)[:]
+        q_final = [keep.tile([P, SLOTS * 2], BF16, name=f"q_final_{h}", tag=f"q_final_{h}", align_bytes=64) for h in range(2)]
 
         half = T // 2
         halves = (slice(0, half), slice(half, T))
@@ -116,22 +116,11 @@ def tile_moe_shr_lin_relu_kernel(tc, xT, w_words, w_scales, b, gate, offs, pos1,
                     COPY,
                 )
 
-        def interleave(a, lo, hi, copy):
-            copy(
-                q_in[a].bitcast(U32).rearrange("p (n u) -> p n u", u=2)[:, lo:hi],
-                gath[a][:].rearrange("p (u n) -> p n u", u=2)[:, lo:hi],
-            )
+        def interleave(dst, a, lo, hi, copy):
+            copy(dst.bitcast(U32).rearrange("p (n u) -> p n u", u=2), gath[a][:].rearrange("p (u n) -> p n u", u=2)[:, lo:hi])
 
-        def vector_interleave(a, lo, hi):
-            nc.vector.tensor_copy(
-                q_in[a].rearrange("p (n u e) -> p n u e", u=2, e=2)[:, lo:hi],
-                gath[a][:].bitcast(BF16).rearrange("p (u n e) -> p n u e", u=2, e=2)[:, lo:hi],
-            )
-
-        def quantize(a, lo, hi):
-            nc.vector.quantize_mx(
-                out=codes[a][:, lo:hi].bitcast(FP8X4), scales=scales[a][:, lo:hi], in_=q_in[a][:, 4 * lo : 4 * hi]
-            )
+        def quantize(src, a, lo, hi):
+            nc.vector.quantize_mx(out=codes[a][:, lo:hi].bitcast(FP8X4), scales=scales[a][:, lo:hi], in_=src)
 
         def multiply(a, e):
             for h in range(2):
@@ -146,10 +135,10 @@ def tile_moe_shr_lin_relu_kernel(tc, xT, w_words, w_scales, b, gate, offs, pos1,
                     stop=(a == SUM_ORDER[-1]),
                 )
 
-        def shared_interleave(a):
+        def shared_interleave(a, copy):
             base, pitch = place[a, 0] * T, (place[a, 2] - place[a, 0]) * T
             words = cast_sb[:, base : base + 2 * pitch].bitcast(U32).rearrange("p (u w) -> p w u", u=2)
-            nc.scalar.copy(s_in[a].bitcast(U32).rearrange("p (w u) -> p w u", u=2), words[:, 0:T])
+            copy(s_in[a].bitcast(U32).rearrange("p (w u) -> p w u", u=2), words[:, 0:T])
 
         def shared_rows(dst, lo, hi):
             nc.scalar.copy(
@@ -177,7 +166,7 @@ def tile_moe_shr_lin_relu_kernel(tc, xT, w_words, w_scales, b, gate, offs, pos1,
             )
 
         for step, (a, t, n_rows) in enumerate(ORDER):
-            copy = nc.scalar.copy if step < 2 else nc.gpsimd.tensor_copy
+            copy = nc.scalar.copy if step in (0, 1, 6) else nc.gpsimd.tensor_copy
             if a == LAST:
                 cast_rows(t, n_rows, copy)
                 gather_rows(t, n_rows)
@@ -193,41 +182,43 @@ def tile_moe_shr_lin_relu_kernel(tc, xT, w_words, w_scales, b, gate, offs, pos1,
                     cast_pairs(a, t, 0, T, copy)
                 gather_pairs(a, t)
         q_early = keep.tile([P, 2 * SLOTS * 4], BF16, name="q_early", tag="raw_2_0", align_bytes=64)
-        s_early = keep.tile([P, (LAST * T + half) * 4], BF16, name="s_early", tag="raw_2_2", align_bytes=64)
+        s_early = keep.tile([P, (2 * T + half) * 4], BF16, name="s_early", tag="raw_2_2", align_bytes=64)
         for a in range(2):
             q_in[a] = q_early[:, a * SLOTS * 4 : (a + 1) * SLOTS * 4]
-        for a in range(LAST):
-            s_in[a] = s_early[:, a * T * 4 : (a + 1) * T * 4]
-        interleave(0, 0, SLOTS, nc.gpsimd.tensor_copy)
-        interleave(1, 0, SLOTS // 2, nc.gpsimd.tensor_copy)
-        vector_interleave(1, SLOTS // 2, SLOTS)
-        interleave(LAST, 0, SLOTS, nc.scalar.copy)
-        shared_interleave(0)
-        interleave(2, 0, SLOTS, nc.scalar.copy)
-        shared_interleave(1)
-        shared_interleave(2)
-        shared_rows(s_early[:, LAST * T * 4 :], 0, half)
+        for a in range(1, LAST):
+            s_in[a] = s_early[:, (a - 1) * T * 4 : a * T * 4]
+        interleave(q_in[0], 0, 0, SLOTS, nc.gpsimd.tensor_copy)
+        interleave(q_in[1], 1, 0, SLOTS, nc.gpsimd.tensor_copy)
+        s_in[0] = keep.tile([P, T * 4], BF16, name="s_first", tag="raw_1_0", align_bytes=64)[:]
+        shared_interleave(0, nc.gpsimd.tensor_copy)
+        interleave(q_in[LAST], LAST, 0, SLOTS, nc.scalar.copy)
+        shared_interleave(1, nc.scalar.copy)
+        for h in range(2):
+            interleave(q_final[h][:], 2, h * SLOTS // 2, (h + 1) * SLOTS // 2, nc.scalar.copy)
+        shared_interleave(2, nc.scalar.copy)
+        shared_rows(s_early[:, 2 * T * 4 :], 0, half)
         codes[LAST] = keep.tile([P, SLOTS], U32, name="codes_last", tag="gath_1", align_bytes=64)
         for a in SUM_ORDER[:-1]:
-            quantize(a, 0, SLOTS)
+            quantize(q_in[a], a, 0, SLOTS)
             for e in range(E):
                 multiply(a, e)
+        codes[2] = keep.tile([P, SLOTS], U32, name="codes_2", tag="raw_2_0", align_bytes=64)
         for e in range(E):
             if e % 2 == 0:
-                quantize(SUM_ORDER[-1], e * C, (e + 2) * C)
+                quantize(q_final[e // 2][:], SUM_ORDER[-1], e * C, (e + 2) * C)
             multiply(SUM_ORDER[-1], e)
             for h in range(2):
                 nc.scalar.activation(
                     y_sb[:, e * C + h * N : e * C + (h + 1) * N], banks[2 * e + h][:], RELU, bias=b_sb[:, e : e + 1]
                 )
-        s_codes = keep.tile([P, PASSES * T], U32, name="s_codes", tag="q_in_2", align_bytes=64)
-        s_late = keep.tile([P, half * 4], BF16, name="s_late", tag="codes_2", align_bytes=64)
+        s_codes = keep.tile([P, PASSES * T], U32, name="s_codes", tag="q_final_0", align_bytes=64)
+        s_late = keep.tile([P, half * 4], BF16, name="s_late", tag="raw_2_0", align_bytes=64)
         shared_rows(s_late[:], half, T)
         shared = psum.tile([P, T], F32, name="shared", tag="bank0")
         for a in range(LAST):
             shared_quantize(a)
             shared_multiply(a)
-        shared_quantize_last(s_early[:, LAST * T * 4 :], 0, half)
+        shared_quantize_last(s_early[:, 2 * T * 4 :], 0, half)
 
         first = keep.tile([P, T], F32, name="first")
         partial = keep.tile([P, T], F32, name="partial")
@@ -240,9 +231,10 @@ def tile_moe_shr_lin_relu_kernel(tc, xT, w_words, w_scales, b, gate, offs, pos1,
         shared_quantize_last(s_late[:], half, T)
         shared_multiply(LAST)
         nc.scalar.activation(ys_sb[:], shared[:], RELU, bias=b_sb[:, E : E + 1])
-        second = keep.tile([P, T], F32, name="second", tag="codes_2", align_bytes=64)
+        second = keep.tile([P, T], F32, name="second", tag="raw_last")
         pick(second[:], 1, pos2_sb, 0, T)
-        nc.vector.tensor_add(partial[:], first[:], ys_sb[:])
+        for cols in halves:
+            nc.vector.tensor_add(partial[:, cols], first[:, cols], ys_sb[:, cols])
         for cols in halves:
             nc.vector.tensor_add(total[:, cols], partial[:, cols], second[:, cols])
             nc.sync.dma_start(out[:, cols], total[:, cols])

@@ -23,7 +23,6 @@ SLOTS = E * C
 ROWS = 4 * PASSES
 ORDER = ((0, 2, 2), (LAST, 3, 1), (0, 0, 2), (LAST, 2, 1), (1, 2, 2), (1, 0, 2), (LAST, 0, 2), (2, 2, 2), (2, 0, 2))
 SUM_ORDER = (0, 1, LAST, 2)
-PIECES = {1: ((0, 384), (384, 768), (768, 1024)), 2: ((0, 768), (768, 1024)), 3: ((0, 1024),)}
 
 FLOPS = 2 * K * N * (SLOTS + T)
 
@@ -44,7 +43,7 @@ def tile_moe_shr_lin_relu_kernel(tc, xT, w_words, w_scales, b, gate, offs, pos1,
         y_sb = keep.tile([P, SLOTS], F32, name="y_sb")
         ys_sb = keep.tile([P, T], F32, name="ys_sb")
         banks = [psum.tile([P, N], F32, name=f"bank{i}", tag=f"bank{i}") for i in range(8)]
-        cast_sb = keep.tile([P, (ROWS + 1) * T], BF16, name="cast_sb", align_bytes=64)
+        cast_sb = keep.tile([P, (ROWS + 4) * T], BF16, name="cast_sb", align_bytes=64)
         raw, gath, q_in, codes, scales = {}, {}, {}, {}, {}
         s_in, s_scales = {}, {}
         raw_last = keep.tile([P, 4, T], F32, name="raw_last", tag="raw_last")
@@ -54,6 +53,8 @@ def tile_moe_shr_lin_relu_kernel(tc, xT, w_words, w_scales, b, gate, offs, pos1,
             place[a, t] = top
             if a == LAST:
                 raw[a, t] = raw_last[:, t : t + n_rows]
+            elif top + n_rows == ROWS:
+                raw[a, t] = cast_sb[:, ROWS * T :].bitcast(F32).rearrange("p (e w) -> p e w", e=2)
             else:
                 raw[a, t] = keep.tile([P, 2, T], F32, name=f"raw_{a}_{t}", tag=f"raw_{a}_{t}", align_bytes=64)[:]
         for a in range(PASSES):
@@ -95,13 +96,8 @@ def tile_moe_shr_lin_relu_kernel(tc, xT, w_words, w_scales, b, gate, offs, pos1,
             )
 
         def gather_pairs(a, t):
-            n_pairs = min(3, (ROWS - place[a, t]) // 2)
-            window = cast_sb[:, place[a, t] * T : (place[a, t] + 2 * n_pairs) * T].bitcast(U32)
-            for lo, hi in PIECES[n_pairs]:
-                nc.vector.tensor_copy(
-                    gath[a][:, t // 2 * SLOTS + lo : t // 2 * SLOTS + hi],
-                    window.indirect(offs_sb[:, lo // 16 : hi // 16]),
-                )
+            window = cast_sb[:, place[a, t] * T : (place[a, t] + 6) * T].bitcast(U32)
+            nc.vector.tensor_copy(gath[a][:, t // 2 * SLOTS : (t // 2 + 1) * SLOTS], window.indirect(offs_sb[:]))
 
         def cast_rows(t, n_rows, copy):
             base = place[LAST, t] * T
@@ -230,11 +226,13 @@ def tile_moe_shr_lin_relu_kernel(tc, xT, w_words, w_scales, b, gate, offs, pos1,
         pick(first[:], 0, pos1_sb, 0, T)
         shared_quantize_last(s_late[:], half, T)
         shared_multiply(LAST)
-        nc.scalar.activation(ys_sb[:], shared[:], RELU, bias=b_sb[:, E : E + 1])
+        for cols in halves:
+            nc.scalar.activation(ys_sb[:, cols], shared[:, cols], RELU, bias=b_sb[:, E : E + 1])
         second = keep.tile([P, T], F32, name="second", tag="raw_last")
-        pick(second[:], 1, pos2_sb, 0, T)
         for cols in halves:
-            nc.vector.tensor_add(partial[:, cols], first[:, cols], ys_sb[:, cols])
+            pick(second[:, cols], 1, pos2_sb, cols.start, cols.stop)
         for cols in halves:
-            nc.vector.tensor_add(total[:, cols], partial[:, cols], second[:, cols])
+            nc.vector.tensor_add(partial[:, cols], first[:, cols], second[:, cols])
+        for cols in halves:
+            nc.vector.tensor_add(total[:, cols], partial[:, cols], ys_sb[:, cols])
             nc.sync.dma_start(out[:, cols], total[:, cols])

@@ -68,12 +68,13 @@ def tile_moe_shr_lin_relu_kernel(tc, xT, w_words, w_scales, b, gate, offs, pos1,
 
         half = T // 2
         halves = (slice(0, half), slice(half, T))
+        thirds = (slice(0, 128), slice(128, 320), slice(320, T))
         nc.vector.memset(ws_sb[:].rearrange("p g n -> p (g n)").bitcast(I32), 0)
 
         for step, (a, t, n_rows) in enumerate(ORDER):
             rows = xT[a * K_PASS : (a + 1) * K_PASS, :].rearrange("(p t) w -> p t w", t=4)
             if a == 0:
-                for cols in halves:
+                for cols in halves if step == 0 else thirds:
                     nc.sync.dma_start(raw[a, t][:, :, cols], rows[:, t : t + n_rows, cols])
             else:
                 nc.sync.dma_start(raw[a, t], rows[:, t : t + n_rows])
@@ -150,13 +151,13 @@ def tile_moe_shr_lin_relu_kernel(tc, xT, w_words, w_scales, b, gate, offs, pos1,
         def shared_quantize(a):
             nc.vector.quantize_mx(out=s_codes[:, a * T : (a + 1) * T].bitcast(FP8X4), scales=s_scales[a][:], in_=s_in[a])
 
-        def shared_multiply(a):
+        def shared_multiply(a, j):
             nc.tensor.matmul_mx(
-                out=shared[:],
+                out=shared[j][:],
                 lhsT=w_sb[:, E * PASSES + a, :].bitcast(FP4X4),
                 lhsT_scale=ws_sb[:, E * PASSES + a, :],
-                rhs=s_codes[:, a * T : (a + 1) * T].bitcast(FP8X4),
-                rhs_scale=s_scales[a][:],
+                rhs=s_codes[:, a * T + j * N : a * T + (j + 1) * N].bitcast(FP8X4),
+                rhs_scale=s_scales[a][:, j * N : (j + 1) * N],
                 start=(a == 0),
                 stop=(a == LAST),
             )
@@ -172,13 +173,13 @@ def tile_moe_shr_lin_relu_kernel(tc, xT, w_words, w_scales, b, gate, offs, pos1,
                     cast_pairs(a, t, half, 416, nc.vector.tensor_copy)
                     cast_pairs(a, t, 416, T, copy)
                 elif a == 0:
-                    cast_pairs(a, t, 0, half, copy)
-                    cast_pairs(a, t, half, T, copy)
+                    for cols in thirds:
+                        cast_pairs(a, t, cols.start, cols.stop, copy)
                 else:
                     cast_pairs(a, t, 0, T, copy)
                 gather_pairs(a, t)
         q_early = keep.tile([P, 2 * SLOTS * 4], BF16, name="q_early", tag="raw_2_0", align_bytes=64)
-        s_early = keep.tile([P, (2 * T + half) * 4], BF16, name="s_early", tag="raw_2_2", align_bytes=64)
+        s_early = keep.tile([P, (2 * T + N) * 4], BF16, name="s_early", tag="raw_2_2", align_bytes=64)
         for a in range(2):
             q_in[a] = q_early[:, a * SLOTS * 4 : (a + 1) * SLOTS * 4]
         for a in range(1, LAST):
@@ -192,7 +193,7 @@ def tile_moe_shr_lin_relu_kernel(tc, xT, w_words, w_scales, b, gate, offs, pos1,
         for h in range(2):
             interleave(q_final[h][:], 2, h * SLOTS // 2, (h + 1) * SLOTS // 2, nc.scalar.copy)
         shared_interleave(2, nc.scalar.copy)
-        shared_rows(s_early[:, 2 * T * 4 :], 0, half)
+        shared_rows(s_early[:, 2 * T * 4 :], 0, N)
         codes[LAST] = keep.tile([P, SLOTS], U32, name="codes_last", tag="gath_1", align_bytes=64)
         for a in SUM_ORDER[:-1]:
             quantize(q_in[a], a, 0, SLOTS)
@@ -208,31 +209,36 @@ def tile_moe_shr_lin_relu_kernel(tc, xT, w_words, w_scales, b, gate, offs, pos1,
                     y_sb[:, e * C + h * N : e * C + (h + 1) * N], banks[2 * e + h][:], RELU, bias=b_sb[:, e : e + 1]
                 )
         s_codes = keep.tile([P, PASSES * T], U32, name="s_codes", tag="q_final_0", align_bytes=64)
-        s_late = keep.tile([P, half * 4], BF16, name="s_late", tag="raw_2_0", align_bytes=64)
-        shared_rows(s_late[:], half, T)
-        shared = psum.tile([P, T], F32, name="shared", tag="bank0")
+        s_late = keep.tile([P, (T - N) * 4], BF16, name="s_late", tag="raw_2_0", align_bytes=64)
+        shared_rows(s_late[:, 0 : 4 * N], N, half)
+        shared_rows(s_late[:, 4 * N :], half, T)
+        shared = [psum.tile([P, N], F32, name=f"shared{j}", tag=f"bank{j}") for j in range(T // N)]
         for a in range(LAST):
             shared_quantize(a)
-            shared_multiply(a)
-        shared_quantize_last(s_early[:, 2 * T * 4 :], 0, half)
+            for j in range(T // N):
+                shared_multiply(a, j)
+        shared_quantize_last(s_early[:, 2 * T * 4 :], 0, N)
 
         first = keep.tile([P, T], F32, name="first")
-        partial = keep.tile([P, T], F32, name="partial")
         total = keep.tile([P, T], F32, name="total")
 
         def pick(dst, r, lst, lo, hi):
             nc.vector.tensor_tensor(dst, y_sb[:].indirect(lst[:, lo // 16 : hi // 16]), gate_sb[:, r, lo:hi], MULT)
 
         pick(first[:], 0, pos1_sb, 0, T)
-        shared_quantize_last(s_late[:], half, T)
-        shared_multiply(LAST)
-        for cols in halves:
-            nc.scalar.activation(ys_sb[:, cols], shared[:, cols], RELU, bias=b_sb[:, E : E + 1])
-        second = keep.tile([P, T], F32, name="second", tag="raw_last")
-        for cols in halves:
-            pick(second[:, cols], 1, pos2_sb, cols.start, cols.stop)
-        for cols in halves:
-            nc.vector.tensor_add(partial[:, cols], first[:, cols], second[:, cols])
+        second = [keep.tile([P, half], F32, name="second_0")[:]]
+        shared_quantize_last(s_late[:, 0 : 4 * N], N, half)
+        pick(second[0], 1, pos2_sb, 0, half)
+        shared_quantize_last(s_late[:, 4 * N :], half, T)
+        for j in range(T // N):
+            shared_multiply(LAST, j)
+            nc.scalar.activation(ys_sb[:, j * N : (j + 1) * N], shared[j][:], RELU, bias=b_sb[:, E : E + 1])
+        held = keep.tile([P, half + T], F32, name="held", tag="raw_last")
+        second.append(held[:, 0:half])
+        partial = held[:, half:]
+        pick(second[1], 1, pos2_sb, half, T)
+        for h, cols in enumerate(halves):
+            nc.vector.tensor_add(partial[:, cols], first[:, cols], second[h])
         for cols in halves:
             nc.vector.tensor_add(total[:, cols], partial[:, cols], ys_sb[:, cols])
             nc.sync.dma_start(out[:, cols], total[:, cols])

@@ -24,6 +24,8 @@ ROWS = 4 * PASSES
 ORDER = ((0, 2, 2), (LAST, 3, 1), (0, 0, 2), (LAST, 2, 1), (1, 2, 2), (1, 0, 2), (LAST, 0, 2), (2, 2, 2), (2, 0, 2))
 SUM_ORDER = (0, 1, LAST, 2)
 
+SCALAR_SLOTS = 128
+
 FLOPS = 2 * K * N * (SLOTS + T)
 
 
@@ -64,6 +66,7 @@ def tile_moe_shr_lin_relu_kernel(tc, xT, w_words, w_scales, b, gate, offs, pos1,
                 codes[a] = keep.tile([P, SLOTS], U32, name=f"codes_{a}", align_bytes=64)
             gath[a] = keep.tile([P, 2 * SLOTS], U32, name=f"gath_{a}", tag=f"gath_{a}", align_bytes=64)
         q_in[LAST] = keep.tile([P, SLOTS * 4], BF16, name="q_in_last", align_bytes=64)[:]
+        first_rows = keep.tile([P, 2, T], BF16, name="first_rows", align_bytes=64)
         q_final = [keep.tile([P, SLOTS * 2], BF16, name=f"q_final_{h}", tag=f"q_final_{h}", align_bytes=64) for h in range(2)]
 
         half = T // 2
@@ -96,16 +99,26 @@ def tile_moe_shr_lin_relu_kernel(tc, xT, w_words, w_scales, b, gate, offs, pos1,
                 raw[a, t][:, :, lo:hi].rearrange("p e w -> p w e"),
             )
 
-        def gather_pairs(a, t):
+        def gather_pairs(a, t, lo):
             window = cast_sb[:, place[a, t] * T : (place[a, t] + 6) * T].bitcast(U32)
-            nc.vector.tensor_copy(gath[a][:, t // 2 * SLOTS : (t // 2 + 1) * SLOTS], window.indirect(offs_sb[:]))
+            nc.vector.tensor_copy(gath[a][:, t // 2 * SLOTS + lo : (t // 2 + 1) * SLOTS], window.indirect(offs_sb[:, lo // 16 :]))
+
+        def cast_first_rows(a, t):
+            for cols in halves:
+                nc.scalar.copy(first_rows[:, :, cols], raw[a, t][:, :, cols])
+
+        def gather_first_rows(a, t):
+            words = gath[a][:, t // 2 * SLOTS : t // 2 * SLOTS + SCALAR_SLOTS].bitcast(BF16).rearrange("p (n e) -> p n e", e=2)
+            for e in range(2):
+                nc.scalar.activation(words[:, :, e], first_rows[:, e].indirect(offs_sb[:, 0 : SCALAR_SLOTS // 16]), COPY)
 
         def cast_rows(t, n_rows, copy):
-            base = place[LAST, t] * T
-            copy(cast_sb[:, base : base + n_rows * T], raw[LAST, t].rearrange("p e w -> p (e w)"))
+            for e in reversed(range(n_rows)):
+                base = (place[LAST, t] + e) * T
+                copy(cast_sb[:, base : base + T], raw[LAST, t][:, e])
 
         def gather_rows(t, n_rows):
-            for e in range(n_rows):
+            for e in reversed(range(n_rows)):
                 base = (place[LAST, t] + e) * T
                 nc.scalar.activation(
                     gath[LAST][:].bitcast(BF16).rearrange("p (u n e) -> p u n e", u=2, e=2)[:, (t + e) // 2, :, (t + e) % 2],
@@ -163,21 +176,23 @@ def tile_moe_shr_lin_relu_kernel(tc, xT, w_words, w_scales, b, gate, offs, pos1,
             )
 
         for step, (a, t, n_rows) in enumerate(ORDER):
-            copy = nc.scalar.copy if step in (0, 1, 6) else nc.gpsimd.tensor_copy
+            copy = nc.scalar.copy if step in (1, 6) else nc.gpsimd.tensor_copy
             if a == LAST:
                 cast_rows(t, n_rows, copy)
+                if step == 1:
+                    gather_first_rows(*ORDER[0][:2])
                 gather_rows(t, n_rows)
             else:
                 if step == 0:
-                    cast_pairs(a, t, 0, half, nc.vector.tensor_copy)
-                    cast_pairs(a, t, half, 416, nc.vector.tensor_copy)
-                    cast_pairs(a, t, 416, T, copy)
+                    for cols in halves:
+                        cast_pairs(a, t, cols.start, cols.stop, nc.vector.tensor_copy)
+                    cast_first_rows(a, t)
                 elif a == 0:
                     for cols in thirds:
                         cast_pairs(a, t, cols.start, cols.stop, copy)
                 else:
                     cast_pairs(a, t, 0, T, copy)
-                gather_pairs(a, t)
+                gather_pairs(a, t, SCALAR_SLOTS if step == 0 else 0)
         q_early = keep.tile([P, 2 * SLOTS * 4], BF16, name="q_early", tag="raw_2_0", align_bytes=64)
         s_early = keep.tile([P, (2 * T + N) * 4], BF16, name="s_early", tag="raw_2_2", align_bytes=64)
         for a in range(2):
@@ -188,8 +203,8 @@ def tile_moe_shr_lin_relu_kernel(tc, xT, w_words, w_scales, b, gate, offs, pos1,
         interleave(q_in[1], 1, 0, SLOTS, nc.gpsimd.tensor_copy)
         s_in[0] = keep.tile([P, T * 4], BF16, name="s_first", tag="raw_1_0", align_bytes=64)[:]
         shared_interleave(0, nc.gpsimd.tensor_copy)
-        interleave(q_in[LAST], LAST, 0, SLOTS, nc.scalar.copy)
         shared_interleave(1, nc.scalar.copy)
+        interleave(q_in[LAST], LAST, 0, SLOTS, nc.scalar.copy)
         for h in range(2):
             interleave(q_final[h][:], 2, h * SLOTS // 2, (h + 1) * SLOTS // 2, nc.scalar.copy)
         shared_interleave(2, nc.scalar.copy)

@@ -77,11 +77,12 @@ def tile_moe_shr_lin_relu_kernel(tc, xT, w_words, w_scales, b, gate, offs, pos1,
         for step, (a, t, n_rows) in enumerate(ORDER):
             rows = xT[a * K_PASS : (a + 1) * K_PASS, :].rearrange("(p t) w -> p t w", t=4)
             if a == 0:
-                for cols in halves if step == 0 else thirds:
+                for cols in halves if step == 0 else thirds[1:]:
                     nc.sync.dma_start(raw[a, t][:, :, cols], rows[:, t : t + n_rows, cols])
             else:
                 nc.sync.dma_start(raw[a, t], rows[:, t : t + n_rows])
             if step == 0:
+                nc.sync.dma_start(raw[0, 0][:, :, thirds[0]], rows[:, 0:2, thirds[0]])
                 nc.sync.dma_start(offs_sb[:], offs)
         nc.sync.dma_start(w_sb[:].bitcast(I32), w_words.rearrange("e a p n -> p (e a) n").bitcast(I32))
         scale_rows = w_scales.rearrange("e a q n -> q (e a) n").bitcast(I32)
@@ -104,13 +105,13 @@ def tile_moe_shr_lin_relu_kernel(tc, xT, w_words, w_scales, b, gate, offs, pos1,
             nc.vector.tensor_copy(gath[a][:, t // 2 * SLOTS + lo : (t // 2 + 1) * SLOTS], window.indirect(offs_sb[:, lo // 16 :]))
 
         def cast_first_rows(a, t):
-            for cols in halves:
-                nc.scalar.copy(first_rows[:, :, cols], raw[a, t][:, :, cols])
-
-        def gather_first_rows(a, t):
-            words = gath[a][:, t // 2 * SLOTS : t // 2 * SLOTS + SCALAR_SLOTS].bitcast(BF16).rearrange("p (n e) -> p n e", e=2)
+            nc.scalar.copy(first_rows[:, :, halves[0]], raw[a, t][:, :, halves[0]])
             for e in range(2):
-                nc.scalar.activation(words[:, :, e], first_rows[:, e].indirect(offs_sb[:, 0 : SCALAR_SLOTS // 16]), COPY)
+                nc.scalar.copy(first_rows[:, e, halves[1]], raw[a, t][:, e, halves[1]])
+
+        def gather_first_row(a, t, e):
+            words = gath[a][:, t // 2 * SLOTS : t // 2 * SLOTS + SCALAR_SLOTS].bitcast(BF16).rearrange("p (n e) -> p n e", e=2)
+            nc.scalar.activation(words[:, :, e], first_rows[:, e].indirect(offs_sb[:, 0 : SCALAR_SLOTS // 16]), COPY)
 
         def cast_rows(t, n_rows, copy):
             for e in reversed(range(n_rows)):
@@ -180,15 +181,17 @@ def tile_moe_shr_lin_relu_kernel(tc, xT, w_words, w_scales, b, gate, offs, pos1,
             if a == LAST:
                 cast_rows(t, n_rows, copy)
                 if step == 1:
-                    gather_first_rows(*ORDER[0][:2])
+                    gather_first_row(*ORDER[0][:2], 1)
                 gather_rows(t, n_rows)
             else:
                 if step == 0:
                     for cols in halves:
                         cast_pairs(a, t, cols.start, cols.stop, nc.vector.tensor_copy)
+                    cast_pairs(0, 0, thirds[0].start, thirds[0].stop, nc.vector.tensor_copy)
                     cast_first_rows(a, t)
+                    gather_first_row(a, t, 0)
                 elif a == 0:
-                    for cols in thirds:
+                    for cols in thirds[1:]:
                         cast_pairs(a, t, cols.start, cols.stop, copy)
                 else:
                     cast_pairs(a, t, 0, T, copy)

@@ -153,8 +153,8 @@ def tile_moe_shr_lin_relu_kernel(tc, xT, w_words, w_scales, b, gate, offs, pos1,
 
         def shared_rows(dst, lo, hi):
             nc.scalar.copy(
-                dst.rearrange("p (c i t) -> p c t i", i=4, t=4),
-                raw_last[:, :, lo:hi].rearrange("p t (c i) -> p c t i", i=4),
+                dst.rearrange("p (c i t) -> p c t i", i=2, t=4),
+                raw_last[:, :, lo:hi].rearrange("p t (c i) -> p c t i", i=2),
             )
 
         def shared_quantize_last(src, lo, hi):

@@ -44,7 +44,7 @@ def tile_moe_shr_lin_relu_kernel(tc, xT, w_words, w_scales, b, gate, offs, pos1,
         gate_sb = keep.tile([P, 2, T], F32, name="gate_sb")
         y_sb = keep.tile([P, SLOTS], F32, name="y_sb")
         ys_sb = keep.tile([P, T], F32, name="ys_sb")
-        banks = [psum.tile([P, N], F32, name=f"bank{i}", tag=f"bank{i}") for i in range(8)]
+        banks = [psum.tile([P, C], F32, name=f"bank{e}", tag=f"bank{e}") for e in range(E)]
         cast_sb = keep.tile([P, (ROWS + 4) * T], BF16, name="cast_sb", align_bytes=64)
         raw, gath, q_in, codes, scales = {}, {}, {}, {}, {}
         s_in, s_scales = {}, {}
@@ -137,13 +137,13 @@ def tile_moe_shr_lin_relu_kernel(tc, xT, w_words, w_scales, b, gate, offs, pos1,
             for h in range(2):
                 cols = slice(e * C + h * N, e * C + (h + 1) * N)
                 nc.tensor.matmul_mx(
-                    out=banks[2 * e + h][:],
+                    out=banks[e][:, h * N : (h + 1) * N],
                     lhsT=w_sb[:, e * PASSES + a, :].bitcast(FP4X4),
                     lhsT_scale=ws_sb[:, e * PASSES + a, :],
                     rhs=codes[a][:, cols].bitcast(FP8X4),
                     rhs_scale=scales[a][:, cols],
-                    start=(a == SUM_ORDER[0]),
-                    stop=(a == SUM_ORDER[-1]),
+                    start=(a == SUM_ORDER[0] and h == 0),
+                    stop=(a == SUM_ORDER[-1] and h == 1),
                 )
 
         def shared_interleave(a, copy):
@@ -197,7 +197,7 @@ def tile_moe_shr_lin_relu_kernel(tc, xT, w_words, w_scales, b, gate, offs, pos1,
                     cast_pairs(a, t, 0, T, copy)
                 gather_pairs(a, t, SCALAR_SLOTS if step == 0 else 0)
         q_early = keep.tile([P, 2 * SLOTS * 4], BF16, name="q_early", tag="raw_2_0", align_bytes=64)
-        s_early = keep.tile([P, (2 * T + N) * 4], BF16, name="s_early", tag="raw_2_2", align_bytes=64)
+        s_early = keep.tile([P, 2 * T * 4], BF16, name="s_early", tag="raw_2_2", align_bytes=64)
         for a in range(2):
             q_in[a] = q_early[:, a * SLOTS * 4 : (a + 1) * SLOTS * 4]
         for a in range(1, LAST):
@@ -211,7 +211,6 @@ def tile_moe_shr_lin_relu_kernel(tc, xT, w_words, w_scales, b, gate, offs, pos1,
         for h in range(2):
             interleave(q_final[h][:], 2, h * SLOTS // 2, (h + 1) * SLOTS // 2, nc.scalar.copy)
         shared_interleave(2, nc.scalar.copy)
-        shared_rows(s_early[:, 2 * T * 4 :], 0, N)
         codes[LAST] = keep.tile([P, SLOTS], U32, name="codes_last", tag="gath_1", align_bytes=64)
         for a in SUM_ORDER[:-1]:
             quantize(q_in[a], a, 0, SLOTS)
@@ -222,20 +221,16 @@ def tile_moe_shr_lin_relu_kernel(tc, xT, w_words, w_scales, b, gate, offs, pos1,
             if e % 2 == 0:
                 quantize(q_final[e // 2][:], SUM_ORDER[-1], e * C, (e + 2) * C)
             multiply(SUM_ORDER[-1], e)
-            for h in range(2):
-                nc.scalar.activation(
-                    y_sb[:, e * C + h * N : e * C + (h + 1) * N], banks[2 * e + h][:], RELU, bias=b_sb[:, e : e + 1]
-                )
+            nc.scalar.activation(y_sb[:, e * C : (e + 1) * C], banks[e][:], RELU, bias=b_sb[:, e : e + 1])
         s_codes = keep.tile([P, PASSES * T], U32, name="s_codes", tag="q_final_0", align_bytes=64)
-        s_late = keep.tile([P, (T - N) * 4], BF16, name="s_late", tag="raw_2_0", align_bytes=64)
-        shared_rows(s_late[:, 0 : 4 * N], N, half)
-        shared_rows(s_late[:, 4 * N :], half, T)
-        shared = [psum.tile([P, N], F32, name=f"shared{j}", tag=f"bank{j}") for j in range(T // N)]
+        s_late = keep.tile([P, T * 4], BF16, name="s_late", tag="raw_2_0", align_bytes=64)
+        for cols in halves:
+            shared_rows(s_late[:, 4 * cols.start : 4 * cols.stop], cols.start, cols.stop)
+        shared = [psum.tile([P, N], F32, name=f"shared{j}", tag=f"shared{j}") for j in range(T // N)]
         for a in range(LAST):
             shared_quantize(a)
             for j in range(T // N):
                 shared_multiply(a, j)
-        shared_quantize_last(s_early[:, 2 * T * 4 :], 0, N)
 
         first = keep.tile([P, T], F32, name="first")
         total = keep.tile([P, T], F32, name="total")
@@ -245,9 +240,9 @@ def tile_moe_shr_lin_relu_kernel(tc, xT, w_words, w_scales, b, gate, offs, pos1,
 
         pick(first[:], 0, pos1_sb, 0, T)
         second = [keep.tile([P, half], F32, name="second_0")[:]]
-        shared_quantize_last(s_late[:, 0 : 4 * N], N, half)
+        shared_quantize_last(s_late[:, 0 : 4 * half], 0, half)
         pick(second[0], 1, pos2_sb, 0, half)
-        shared_quantize_last(s_late[:, 4 * N :], half, T)
+        shared_quantize_last(s_late[:, 4 * half :], half, T)
         for j in range(T // N):
             shared_multiply(LAST, j)
             nc.scalar.activation(ys_sb[:, j * N : (j + 1) * N], shared[j][:], RELU, bias=b_sb[:, E : E + 1])

@@ -20,11 +20,12 @@ K_PASS = 512
 PASSES = K // K_PASS
 LAST = PASSES - 1
 SLOTS = E * C
-ROWS = 4 * PASSES
-ORDER = ((0, 2, 2), (LAST, 3, 1), (0, 0, 2), (LAST, 2, 1), (1, 2, 2), (1, 0, 2), (LAST, 0, 2), (2, 2, 2), (2, 0, 2))
+HALF = T // 2
+HALVES = (slice(0, HALF), slice(HALF, T))
+SCALAR_SLOTS = 448
+SCALAR_PIECE = slice(448, T)
+GPSIMD_PIECES = (slice(0, 224), slice(224, 448))
 SUM_ORDER = (0, 1, LAST, 2)
-
-SCALAR_SLOTS = 128
 
 FLOPS = 2 * K * N * (SLOTS + T)
 
@@ -35,55 +36,57 @@ def tile_moe_shr_lin_relu_kernel(tc, xT, w_words, w_scales, b, gate, offs, pos1,
         keep = ctx.enter_context(tc.tile_pool(name="keep", bufs=1))
         psum = ctx.enter_context(tc.psum_pool(name="psum", bufs=1))
 
-        offs_sb = keep.tile([P, SLOTS // 16], U16, name="offs_sb")
-        pos1_sb = keep.tile([P, T // 16], U16, name="pos1_sb")
-        pos2_sb = keep.tile([P, T // 16], U16, name="pos2_sb")
+        def tile(name, width, dtype, tag=None):
+            return keep.tile([P, width], dtype, name=name, tag=tag or name, align_bytes=64)
+
+        offs_sb = tile("offs_sb", SLOTS // 16, U16)
+        pos1_sb = tile("pos1_sb", T // 16, U16)
+        pos2_sb = tile("pos2_sb", T // 16, U16)
         w_sb = keep.tile([P, (E + 1) * PASSES, 2 * N], U8, name="w_sb", align_bytes=64)
         ws_sb = keep.tile([P, (E + 1) * PASSES, N], U8, name="ws_sb", align_bytes=64)
-        b_sb = keep.tile([P, E + 1], F32, name="b_sb")
+        b_sb = tile("b_sb", E + 1, F32)
         gate_sb = keep.tile([P, 2, T], F32, name="gate_sb")
-        y_sb = keep.tile([P, SLOTS], F32, name="y_sb")
-        ys_sb = keep.tile([P, T], F32, name="ys_sb")
+        y_sb = tile("y_sb", SLOTS, F32)
+        ys_sb = tile("ys_sb", T, F32)
         banks = [psum.tile([P, C], F32, name=f"bank{e}", tag=f"bank{e}") for e in range(E)]
-        cast_sb = keep.tile([P, (ROWS + 4) * T], BF16, name="cast_sb", align_bytes=64)
-        raw, gath, q_in, codes, scales = {}, {}, {}, {}, {}
-        s_in, s_scales = {}, {}
-        raw_last = keep.tile([P, 4, T], F32, name="raw_last", tag="raw_last")
-        place, top = {}, ROWS
-        for a, t, n_rows in ORDER:
-            top -= n_rows
-            place[a, t] = top
-            if a == LAST:
-                raw[a, t] = raw_last[:, t : t + n_rows]
-            elif top + n_rows == ROWS:
-                raw[a, t] = cast_sb[:, ROWS * T :].bitcast(F32).rearrange("p (e w) -> p e w", e=2)
-            else:
-                raw[a, t] = keep.tile([P, 2, T], F32, name=f"raw_{a}_{t}", tag=f"raw_{a}_{t}", align_bytes=64)[:]
-        for a in range(PASSES):
-            scales[a] = keep.tile([P, SLOTS], U8, name=f"scales_{a}", align_bytes=64)
-            s_scales[a] = keep.tile([P, T], U8, name=f"s_scales_{a}", align_bytes=64)
-            if a < 2:
-                codes[a] = keep.tile([P, SLOTS], U32, name=f"codes_{a}", align_bytes=64)
-            gath[a] = keep.tile([P, 2 * SLOTS], U32, name=f"gath_{a}", tag=f"gath_{a}", align_bytes=64)
-        q_in[LAST] = keep.tile([P, SLOTS * 4], BF16, name="q_in_last", align_bytes=64)[:]
-        first_rows = keep.tile([P, 2, T], BF16, name="first_rows", align_bytes=64)
-        q_final = [keep.tile([P, SLOTS * 2], BF16, name=f"q_final_{h}", tag=f"q_final_{h}", align_bytes=64) for h in range(2)]
+        shared = [psum.tile([P, N], F32, name=f"shared{j}", tag=f"shared{j}") for j in range(T // N)]
 
-        half = T // 2
-        halves = (slice(0, half), slice(half, T))
-        thirds = (slice(0, 128), slice(128, 320), slice(320, T))
+        x_rows = xT.rearrange("(a p t) w -> a p t w", p=P, t=4)
+        head_rows = [tile(f"head_row{e}", 2 * T, F32) for e in range(2)]
+        last_rows = [tile(f"last_row{t}", 4 * T, F32) for t in range(4)]
+        raw = {(a, u): tile(f"raw_{a}_{u}", 2 * T, F32) for a in range(LAST) for u in range(2) if (a, u) != (0, 1)}
+        planes = [tile(f"planes_{a}", 4 * T, U32) for a in range(LAST)]
+        gath = [tile(f"gath_{a}", 2 * SLOTS, U32) for a in range(PASSES)]
+        scales = [tile(f"scales_{a}", SLOTS, U8) for a in range(PASSES)]
+        s_scales = [tile(f"s_scales_{a}", T, U8) for a in range(PASSES)]
+
         nc.vector.memset(ws_sb[:].rearrange("p g n -> p (g n)").bitcast(I32), 0)
 
-        for step, (a, t, n_rows) in enumerate(ORDER):
-            rows = xT[a * K_PASS : (a + 1) * K_PASS, :].rearrange("(p t) w -> p t w", t=4)
-            if a == 0:
-                for cols in halves if step == 0 else thirds[1:]:
-                    nc.sync.dma_start(raw[a, t][:, :, cols], rows[:, t : t + n_rows, cols])
-            else:
-                nc.sync.dma_start(raw[a, t], rows[:, t : t + n_rows])
-            if step == 0:
-                nc.sync.dma_start(raw[0, 0][:, :, thirds[0]], rows[:, 0:2, thirds[0]])
-                nc.sync.dma_start(offs_sb[:], offs)
+        def raw_pair(a, u, cols):
+            return raw[a, u][:].rearrange("p (e w) -> p e w", e=2)[:, :, cols]
+
+        def load_pair(a, u, cols):
+            nc.sync.dma_start(raw_pair(a, u, cols), x_rows[a, :, 2 * u : 2 * u + 2, cols])
+
+        def load_last_row(t):
+            nc.sync.dma_start(last_rows[t][:, 0:T], x_rows[LAST, :, t])
+
+        whole = slice(0, T)
+        load_pair(0, 0, SCALAR_PIECE)
+        nc.sync.dma_start(head_rows[0][:, 0:T], x_rows[0, :, 2])
+        nc.sync.dma_start(offs_sb[:], offs)
+        for cols in HALVES:
+            nc.sync.dma_start(head_rows[1][:, cols], x_rows[0, :, 3, cols])
+        for cols in GPSIMD_PIECES:
+            load_pair(0, 0, cols)
+        load_last_row(0)
+        load_pair(1, 1, whole)
+        load_pair(1, 0, whole)
+        load_last_row(2)
+        load_pair(2, 1, whole)
+        load_pair(2, 0, whole)
+        load_last_row(1)
+        load_last_row(3)
         nc.sync.dma_start(w_sb[:].bitcast(I32), w_words.rearrange("e a p n -> p (e a) n").bitcast(I32))
         scale_rows = w_scales.rearrange("e a q n -> q (e a) n").bitcast(I32)
         for quad in range(4):
@@ -93,165 +96,135 @@ def tile_moe_shr_lin_relu_kernel(tc, xT, w_words, w_scales, b, gate, offs, pos1,
         nc.sync.dma_start(pos2_sb[:], pos2)
         nc.sync.dma_start(gate_sb[:], gate.rearrange("r n t -> n r t"))
 
-        def cast_pairs(a, t, lo, hi, copy):
-            base = place[a, t] * T
-            copy(
-                cast_sb[:, base + 2 * lo : base + 2 * hi].rearrange("p (w e) -> p w e", e=2),
-                raw[a, t][:, :, lo:hi].rearrange("p e w -> p w e"),
-            )
+        def plane_values(a, u, cols):
+            return planes[a][:, u * T : (u + 1) * T].bitcast(BF16).rearrange("p (w e) -> p w e", e=2)[:, cols]
 
-        def gather_pairs(a, t, lo):
-            window = cast_sb[:, place[a, t] * T : (place[a, t] + 6) * T].bitcast(U32)
-            nc.vector.tensor_copy(gath[a][:, t // 2 * SLOTS + lo : (t // 2 + 1) * SLOTS], window.indirect(offs_sb[:, lo // 16 :]))
+        def cast_pair(a, u, cols, copy):
+            copy(plane_values(a, u, cols), raw_pair(a, u, cols).rearrange("p e w -> p w e"))
 
-        def cast_first_rows(a, t):
-            nc.scalar.copy(first_rows[:, :, halves[0]], raw[a, t][:, :, halves[0]])
-            for e in range(2):
-                nc.scalar.copy(first_rows[:, e, halves[1]], raw[a, t][:, e, halves[1]])
+        def gather_pair(a, u, lo):
+            window = planes[a][:, u * T : (u + 3) * T]
+            nc.vector.tensor_copy(gath[a][:, u * SLOTS + lo : (u + 1) * SLOTS], window.indirect(offs_sb[:, lo // 16 :]))
 
-        def gather_first_row(a, t, e):
-            words = gath[a][:, t // 2 * SLOTS : t // 2 * SLOTS + SCALAR_SLOTS].bitcast(BF16).rearrange("p (n e) -> p n e", e=2)
-            nc.scalar.activation(words[:, :, e], first_rows[:, e].indirect(offs_sb[:, 0 : SCALAR_SLOTS // 16]), COPY)
-
-        def cast_rows(t, n_rows, copy):
-            for e in reversed(range(n_rows)):
-                base = (place[LAST, t] + e) * T
-                copy(cast_sb[:, base : base + T], raw[LAST, t][:, e])
-
-        def gather_rows(t, n_rows):
-            for e in reversed(range(n_rows)):
-                base = (place[LAST, t] + e) * T
-                nc.scalar.activation(
-                    gath[LAST][:].bitcast(BF16).rearrange("p (u n e) -> p u n e", u=2, e=2)[:, (t + e) // 2, :, (t + e) % 2],
-                    cast_sb[:, base : base + 3 * T].indirect(offs_sb[:]),
-                    COPY,
-                )
+        def gather_row(a, t, row_tile, hi):
+            words = gath[a][:, t // 2 * SLOTS : t // 2 * SLOTS + hi].bitcast(BF16).rearrange("p (n e) -> p n e", e=2)
+            nc.scalar.activation(words[:, :, t % 2], row_tile[:].indirect(offs_sb[:, 0 : hi // 16]), COPY)
 
         def interleave(dst, a, lo, hi, copy):
-            copy(dst.bitcast(U32).rearrange("p (n u) -> p n u", u=2), gath[a][:].rearrange("p (u n) -> p n u", u=2)[:, lo:hi])
+            copy(dst[:].bitcast(U32).rearrange("p (n u) -> p n u", u=2), gath[a][:].rearrange("p (u n) -> p n u", u=2)[:, lo:hi])
 
-        def quantize(src, a, lo, hi):
-            nc.vector.quantize_mx(out=codes[a][:, lo:hi].bitcast(FP8X4), scales=scales[a][:, lo:hi], in_=src)
+        def shared_interleave(dst, a, cols, copy):
+            words = planes[a][:, 0 : 2 * T].rearrange("p (u w) -> p w u", u=2)
+            copy(dst.bitcast(U32).rearrange("p (w u) -> p w u", u=2), words[:, cols])
 
-        def multiply(a, e):
-            for h in range(2):
-                cols = slice(e * C + h * N, e * C + (h + 1) * N)
-                nc.tensor.matmul_mx(
-                    out=banks[e][:, h * N : (h + 1) * N],
-                    lhsT=w_sb[:, e * PASSES + a, :].bitcast(FP4X4),
-                    lhsT_scale=ws_sb[:, e * PASSES + a, :],
-                    rhs=codes[a][:, cols].bitcast(FP8X4),
-                    rhs_scale=scales[a][:, cols],
-                    start=(a == SUM_ORDER[0] and h == 0),
-                    stop=(a == SUM_ORDER[-1] and h == 1),
-                )
+        def quantize(dst, plane, src):
+            nc.vector.quantize_mx(out=dst.bitcast(FP8X4), scales=plane, in_=src)
 
-        def shared_interleave(a, copy):
-            base, pitch = place[a, 0] * T, (place[a, 2] - place[a, 0]) * T
-            words = cast_sb[:, base : base + 2 * pitch].bitcast(U32).rearrange("p (u w) -> p w u", u=2)
-            copy(s_in[a].bitcast(U32).rearrange("p (w u) -> p w u", u=2), words[:, 0:T])
+        def multiply(acc, e, a, words, plane, start, stop):
+            nc.tensor.matmul_mx(
+                out=acc,
+                lhsT=w_sb[:, e * PASSES + a, :].bitcast(FP4X4),
+                lhsT_scale=ws_sb[:, e * PASSES + a, :],
+                rhs=words.bitcast(FP8X4),
+                rhs_scale=plane,
+                start=start,
+                stop=stop,
+            )
 
-        def shared_rows(dst, lo, hi):
+        nc.vector.tensor_copy(plane_values(0, 1, whole)[:, :, 0], head_rows[0][:, 0:T])
+        for cols in HALVES:
+            nc.vector.tensor_copy(plane_values(0, 1, cols)[:, :, 1], head_rows[1][:, cols])
+        cast_pair(0, 0, SCALAR_PIECE, nc.scalar.copy)
+        for e in range(2):
+            gather_row(0, 2 + e, head_rows[e], SCALAR_SLOTS)
+        gather_pair(0, 1, SCALAR_SLOTS)
+        for cols in GPSIMD_PIECES:
+            cast_pair(0, 0, cols, nc.gpsimd.tensor_copy)
+        gather_pair(0, 0, 0)
+        s_first = {1: tile("s_first_1", 4 * HALF, BF16)}
+        shared_interleave(s_first[1][:], 0, HALVES[1], nc.gpsimd.tensor_copy)
+        for t in (0, 2, 1, 3):
+            gather_row(LAST, t, last_rows[t], SLOTS)
+        nc.sync.dma_start(last_rows[0][:, T:], x_rows[LAST, :, 1:4].rearrange("p t w -> p (t w)"))
+        for a in range(1, LAST):
+            for u in (1, 0):
+                cast_pair(a, u, whole, nc.gpsimd.tensor_copy)
+                gather_pair(a, u, 0)
+
+        q_early = tile("q_early", 2 * SLOTS * 4, BF16, tag="raw_2_0")
+        q_in = {a: q_early[:, a * SLOTS * 4 : (a + 1) * SLOTS * 4] for a in range(2)}
+        for a in range(2):
+            interleave(q_in[a], a, 0, SLOTS, nc.gpsimd.tensor_copy)
+        s_in = {1: tile("s_in_1", T * 4, BF16, tag="last_row1")[:], 2: tile("s_in_2", T * 4, BF16)[:]}
+        s_first[0] = tile("s_first_0", 4 * HALF, BF16, tag="raw_1_1")
+        shared_interleave(s_first[0][:], 0, HALVES[0], nc.scalar.copy)
+        shared_interleave(s_in[1], 1, whole, nc.scalar.copy)
+        q_in[LAST] = tile("q_last", SLOTS * 4, BF16)[:]
+        interleave(q_in[LAST], LAST, 0, SLOTS, nc.scalar.copy)
+        q_final = [tile(f"q_final_{h}", SLOTS * 2, BF16) for h in range(2)]
+        for h in range(2):
+            interleave(q_final[h], 2, h * SLOTS // 2, (h + 1) * SLOTS // 2, nc.scalar.copy)
+        shared_interleave(s_in[2], 2, whole, nc.scalar.copy)
+
+        codes = {a: tile(f"codes_{a}", SLOTS, U32) for a in range(2)}
+        codes[LAST] = tile("codes_last", SLOTS, U32, tag="gath_1")
+        for a in SUM_ORDER[:-1]:
+            quantize(codes[a][:], scales[a][:], q_in[a])
+            for e in range(E):
+                cols = slice(e * C, (e + 1) * C)
+                multiply(banks[e][:], e, a, codes[a][:, cols], scales[a][:, cols], a == SUM_ORDER[0], False)
+        a = SUM_ORDER[-1]
+        codes[a] = tile("codes_closing", SLOTS, U32, tag="raw_2_0")
+        for e in range(E):
+            cols = slice(e * C, (e + 1) * C)
+            if e % 2 == 0:
+                both = slice(e * C, (e + 2) * C)
+                quantize(codes[a][:, both], scales[a][:, both], q_final[e // 2][:])
+            multiply(banks[e][:], e, a, codes[a][:, cols], scales[a][:, cols], False, True)
+            nc.scalar.activation(y_sb[:, cols], banks[e][:], RELU, bias=b_sb[:, e : e + 1])
+
+        s_codes = tile("s_codes", PASSES * T, U32, tag="q_final_0")
+        s_late = tile("s_late", T * 4, BF16, tag="raw_2_0")
+        for cols in HALVES:
             nc.scalar.copy(
-                dst.rearrange("p (c i t) -> p c t i", i=2, t=4),
-                raw_last[:, :, lo:hi].rearrange("p t (c i) -> p c t i", i=2),
+                s_late[:, 4 * cols.start : 4 * cols.stop].rearrange("p (c i t) -> p c t i", i=2, t=4),
+                last_rows[0][:].rearrange("p (t w) -> p t w", t=4)[:, :, cols].rearrange("p t (c i) -> p c t i", i=2),
             )
 
-        def shared_quantize_last(src, lo, hi):
-            nc.vector.quantize_mx(
-                out=s_codes[:, LAST * T + lo : LAST * T + hi].bitcast(FP8X4), scales=s_scales[LAST][:, lo:hi], in_=src
-            )
-
-        def shared_quantize(a):
-            nc.vector.quantize_mx(out=s_codes[:, a * T : (a + 1) * T].bitcast(FP8X4), scales=s_scales[a][:], in_=s_in[a])
+        def shared_quantize(a, cols, src):
+            quantize(s_codes[:, a * T + cols.start : a * T + cols.stop], s_scales[a][:, cols], src)
 
         def shared_multiply(a, j):
-            nc.tensor.matmul_mx(
-                out=shared[j][:],
-                lhsT=w_sb[:, E * PASSES + a, :].bitcast(FP4X4),
-                lhsT_scale=ws_sb[:, E * PASSES + a, :],
-                rhs=s_codes[:, a * T + j * N : a * T + (j + 1) * N].bitcast(FP8X4),
-                rhs_scale=s_scales[a][:, j * N : (j + 1) * N],
-                start=(a == 0),
-                stop=(a == LAST),
-            )
+            multiply(shared[j][:], E, a, s_codes[:, a * T + j * N : a * T + (j + 1) * N], s_scales[a][:, j * N : (j + 1) * N], a == 0, a == LAST)
 
-        for step, (a, t, n_rows) in enumerate(ORDER):
-            copy = nc.scalar.copy if step in (1, 6) else nc.gpsimd.tensor_copy
-            if a == LAST:
-                cast_rows(t, n_rows, copy)
-                if step == 1:
-                    gather_first_row(*ORDER[0][:2], 1)
-                gather_rows(t, n_rows)
-            else:
-                if step == 0:
-                    for cols in halves:
-                        cast_pairs(a, t, cols.start, cols.stop, nc.vector.tensor_copy)
-                    cast_pairs(0, 0, thirds[0].start, thirds[0].stop, nc.vector.tensor_copy)
-                    cast_first_rows(a, t)
-                    gather_first_row(a, t, 0)
-                elif a == 0:
-                    for cols in thirds[1:]:
-                        cast_pairs(a, t, cols.start, cols.stop, copy)
-                else:
-                    cast_pairs(a, t, 0, T, copy)
-                gather_pairs(a, t, SCALAR_SLOTS if step == 0 else 0)
-        q_early = keep.tile([P, 2 * SLOTS * 4], BF16, name="q_early", tag="raw_2_0", align_bytes=64)
-        s_early = keep.tile([P, 2 * T * 4], BF16, name="s_early", tag="raw_2_2", align_bytes=64)
-        for a in range(2):
-            q_in[a] = q_early[:, a * SLOTS * 4 : (a + 1) * SLOTS * 4]
-        for a in range(1, LAST):
-            s_in[a] = s_early[:, (a - 1) * T * 4 : a * T * 4]
-        interleave(q_in[0], 0, 0, SLOTS, nc.gpsimd.tensor_copy)
-        interleave(q_in[1], 1, 0, SLOTS, nc.gpsimd.tensor_copy)
-        s_in[0] = keep.tile([P, T * 4], BF16, name="s_first", tag="raw_1_0", align_bytes=64)[:]
-        shared_interleave(0, nc.gpsimd.tensor_copy)
-        shared_interleave(1, nc.scalar.copy)
-        interleave(q_in[LAST], LAST, 0, SLOTS, nc.scalar.copy)
         for h in range(2):
-            interleave(q_final[h][:], 2, h * SLOTS // 2, (h + 1) * SLOTS // 2, nc.scalar.copy)
-        shared_interleave(2, nc.scalar.copy)
-        codes[LAST] = keep.tile([P, SLOTS], U32, name="codes_last", tag="gath_1", align_bytes=64)
-        for a in SUM_ORDER[:-1]:
-            quantize(q_in[a], a, 0, SLOTS)
-            for e in range(E):
-                multiply(a, e)
-        codes[2] = keep.tile([P, SLOTS], U32, name="codes_2", tag="raw_2_0", align_bytes=64)
-        for e in range(E):
-            if e % 2 == 0:
-                quantize(q_final[e // 2][:], SUM_ORDER[-1], e * C, (e + 2) * C)
-            multiply(SUM_ORDER[-1], e)
-            nc.scalar.activation(y_sb[:, e * C : (e + 1) * C], banks[e][:], RELU, bias=b_sb[:, e : e + 1])
-        s_codes = keep.tile([P, PASSES * T], U32, name="s_codes", tag="q_final_0", align_bytes=64)
-        s_late = keep.tile([P, T * 4], BF16, name="s_late", tag="raw_2_0", align_bytes=64)
-        for cols in halves:
-            shared_rows(s_late[:, 4 * cols.start : 4 * cols.stop], cols.start, cols.stop)
-        shared = [psum.tile([P, N], F32, name=f"shared{j}", tag=f"shared{j}") for j in range(T // N)]
-        for a in range(LAST):
-            shared_quantize(a)
+            shared_quantize(0, HALVES[h], s_first[h][:])
+            for j in (2 * h, 2 * h + 1):
+                shared_multiply(0, j)
+        for a in range(1, LAST):
+            shared_quantize(a, whole, s_in[a])
             for j in range(T // N):
                 shared_multiply(a, j)
 
-        first = keep.tile([P, T], F32, name="first")
-        total = keep.tile([P, T], F32, name="total")
+        def pick(dst, r, lst, cols):
+            nc.vector.tensor_tensor(dst, y_sb[:].indirect(lst[:, cols.start // 16 : cols.stop // 16]), gate_sb[:, r, cols], MULT)
 
-        def pick(dst, r, lst, lo, hi):
-            nc.vector.tensor_tensor(dst, y_sb[:].indirect(lst[:, lo // 16 : hi // 16]), gate_sb[:, r, lo:hi], MULT)
-
-        pick(first[:], 0, pos1_sb, 0, T)
-        second = [keep.tile([P, half], F32, name="second_0")[:]]
-        shared_quantize_last(s_late[:, 0 : 4 * half], 0, half)
-        pick(second[0], 1, pos2_sb, 0, half)
-        shared_quantize_last(s_late[:, 4 * half :], half, T)
+        first = tile("first", T, F32)
+        total = tile("total", T, F32)
+        pick(first[:], 0, pos1_sb, whole)
+        second = [tile("second_0", HALF, F32)[:]]
+        shared_quantize(LAST, HALVES[0], s_late[:, 0 : 4 * HALF])
+        pick(second[0], 1, pos2_sb, HALVES[0])
+        shared_quantize(LAST, HALVES[1], s_late[:, 4 * HALF :])
         for j in range(T // N):
             shared_multiply(LAST, j)
             nc.scalar.activation(ys_sb[:, j * N : (j + 1) * N], shared[j][:], RELU, bias=b_sb[:, E : E + 1])
-        held = keep.tile([P, half + T], F32, name="held", tag="raw_last")
-        second.append(held[:, 0:half])
-        partial = held[:, half:]
-        pick(second[1], 1, pos2_sb, half, T)
-        for h, cols in enumerate(halves):
+        held = tile("held", HALF + T, F32, tag="last_row0")
+        second.append(held[:, 0:HALF])
+        partial = held[:, HALF:]
+        pick(second[1], 1, pos2_sb, HALVES[1])
+        for h, cols in enumerate(HALVES):
             nc.vector.tensor_add(partial[:, cols], first[:, cols], second[h])
-        for cols in halves:
+        for cols in HALVES:
             nc.vector.tensor_add(total[:, cols], partial[:, cols], ys_sb[:, cols])
             nc.sync.dma_start(out[:, cols], total[:, cols])

@@ -22,9 +22,8 @@ LAST = PASSES - 1
 SLOTS = E * C
 HALF = T // 2
 HALVES = (slice(0, HALF), slice(HALF, T))
-SCALAR_SLOTS = 448
-SCALAR_PIECE = slice(448, T)
-GPSIMD_PIECES = (slice(0, 224), slice(224, 448))
+SCALAR_SLOTS = 352
+SCALAR_TOKENS = 128
 SUM_ORDER = (0, 1, LAST, 2)
 
 FLOPS = 2 * K * N * (SLOTS + T)
@@ -52,9 +51,9 @@ def tile_moe_shr_lin_relu_kernel(tc, xT, w_words, w_scales, b, gate, offs, pos1,
         shared = [psum.tile([P, N], F32, name=f"shared{j}", tag=f"shared{j}") for j in range(T // N)]
 
         x_rows = xT.rearrange("(a p t) w -> a p t w", p=P, t=4)
-        head_rows = [tile(f"head_row{e}", 2 * T, F32) for e in range(2)]
+        again = tile("again", 2 * T, F32)
         last_rows = [tile(f"last_row{t}", 4 * T, F32) for t in range(4)]
-        raw = {(a, u): tile(f"raw_{a}_{u}", 2 * T, F32) for a in range(LAST) for u in range(2) if (a, u) != (0, 1)}
+        raw = {(a, u): tile(f"raw_{a}_{u}", 2 * T, F32) for a in range(LAST) for u in range(2)}
         planes = [tile(f"planes_{a}", 4 * T, U32) for a in range(LAST)]
         gath = [tile(f"gath_{a}", 2 * SLOTS, U32) for a in range(PASSES)]
         scales = [tile(f"scales_{a}", SLOTS, U8) for a in range(PASSES)]
@@ -72,18 +71,17 @@ def tile_moe_shr_lin_relu_kernel(tc, xT, w_words, w_scales, b, gate, offs, pos1,
             nc.sync.dma_start(last_rows[t][:, 0:T], x_rows[LAST, :, t])
 
         whole = slice(0, T)
-        load_pair(0, 0, SCALAR_PIECE)
-        nc.sync.dma_start(head_rows[0][:, 0:T], x_rows[0, :, 2])
+        for cols in HALVES:
+            load_pair(0, 1, cols)
         nc.sync.dma_start(offs_sb[:], offs)
         for cols in HALVES:
-            nc.sync.dma_start(head_rows[1][:, cols], x_rows[0, :, 3, cols])
-        for cols in GPSIMD_PIECES:
             load_pair(0, 0, cols)
         load_last_row(0)
         load_pair(1, 1, whole)
-        load_pair(1, 0, whole)
         load_last_row(2)
+        load_pair(1, 0, whole)
         load_pair(2, 1, whole)
+        nc.sync.dma_start(again[:, 0:T], x_rows[0, :, 3])
         load_pair(2, 0, whole)
         load_last_row(1)
         load_last_row(3)
@@ -106,9 +104,9 @@ def tile_moe_shr_lin_relu_kernel(tc, xT, w_words, w_scales, b, gate, offs, pos1,
             window = planes[a][:, u * T : (u + 3) * T]
             nc.vector.tensor_copy(gath[a][:, u * SLOTS + lo : (u + 1) * SLOTS], window.indirect(offs_sb[:, lo // 16 :]))
 
-        def gather_row(a, t, row_tile, hi):
-            words = gath[a][:, t // 2 * SLOTS : t // 2 * SLOTS + hi].bitcast(BF16).rearrange("p (n e) -> p n e", e=2)
-            nc.scalar.activation(words[:, :, t % 2], row_tile[:].indirect(offs_sb[:, 0 : hi // 16]), COPY)
+        def gather_row(a, t, row_tile, lo, hi):
+            words = gath[a][:, t // 2 * SLOTS + lo : t // 2 * SLOTS + hi].bitcast(BF16).rearrange("p (n e) -> p n e", e=2)
+            nc.scalar.activation(words[:, :, t % 2], row_tile[:].indirect(offs_sb[:, lo // 16 : hi // 16]), COPY)
 
         def interleave(dst, a, lo, hi, copy):
             copy(dst[:].bitcast(U32).rearrange("p (n u) -> p n u", u=2), gath[a][:].rearrange("p (u n) -> p n u", u=2)[:, lo:hi])
@@ -131,20 +129,23 @@ def tile_moe_shr_lin_relu_kernel(tc, xT, w_words, w_scales, b, gate, offs, pos1,
                 stop=stop,
             )
 
-        nc.vector.tensor_copy(plane_values(0, 1, whole)[:, :, 0], head_rows[0][:, 0:T])
         for cols in HALVES:
-            nc.vector.tensor_copy(plane_values(0, 1, cols)[:, :, 1], head_rows[1][:, cols])
-        cast_pair(0, 0, SCALAR_PIECE, nc.scalar.copy)
-        for e in range(2):
-            gather_row(0, 2 + e, head_rows[e], SCALAR_SLOTS)
+            cast_pair(0, 1, slice(cols.start, cols.start + SCALAR_TOKENS), nc.scalar.copy)
+            cast_pair(0, 1, slice(cols.start + SCALAR_TOKENS, cols.stop), nc.vector.tensor_copy)
+        gather_row(0, 2, raw[0, 1], 0, SCALAR_SLOTS)
         gather_pair(0, 1, SCALAR_SLOTS)
-        for cols in GPSIMD_PIECES:
-            cast_pair(0, 0, cols, nc.gpsimd.tensor_copy)
+        for cols, copy in zip(HALVES, (nc.gpsimd.tensor_copy, nc.scalar.copy)):
+            cast_pair(0, 0, cols, copy)
         gather_pair(0, 0, 0)
-        s_first = {1: tile("s_first_1", 4 * HALF, BF16)}
-        shared_interleave(s_first[1][:], 0, HALVES[1], nc.gpsimd.tensor_copy)
-        for t in (0, 2, 1, 3):
-            gather_row(LAST, t, last_rows[t], SLOTS)
+        s_first = tile("s_first", 4 * T, BF16)
+        for cols in HALVES:
+            shared_interleave(s_first[:, 4 * cols.start : 4 * cols.stop], 0, cols, nc.gpsimd.tensor_copy)
+        for t in (0, 2):
+            gather_row(LAST, t, last_rows[t], 0, SLOTS)
+        gather_row(0, 3, again, 0, SCALAR_SLOTS)
+        gather_row(LAST, 1, last_rows[1], 0, SLOTS)
+        for h in range(2):
+            gather_row(LAST, 3, last_rows[3], h * SLOTS // 2, (h + 1) * SLOTS // 2)
         nc.sync.dma_start(last_rows[0][:, T:], x_rows[LAST, :, 1:4].rearrange("p t w -> p (t w)"))
         for a in range(1, LAST):
             for u in (1, 0):
@@ -155,12 +156,12 @@ def tile_moe_shr_lin_relu_kernel(tc, xT, w_words, w_scales, b, gate, offs, pos1,
         q_in = {a: q_early[:, a * SLOTS * 4 : (a + 1) * SLOTS * 4] for a in range(2)}
         for a in range(2):
             interleave(q_in[a], a, 0, SLOTS, nc.gpsimd.tensor_copy)
-        s_in = {1: tile("s_in_1", T * 4, BF16, tag="last_row1")[:], 2: tile("s_in_2", T * 4, BF16)[:]}
-        s_first[0] = tile("s_first_0", 4 * HALF, BF16, tag="raw_1_1")
-        shared_interleave(s_first[0][:], 0, HALVES[0], nc.scalar.copy)
+        s_in = {1: tile("s_in_1", T * 4, BF16)[:], 2: tile("s_in_2", T * 4, BF16)[:]}
+        s_in[0] = s_first[:]
         shared_interleave(s_in[1], 1, whole, nc.scalar.copy)
         q_in[LAST] = tile("q_last", SLOTS * 4, BF16)[:]
-        interleave(q_in[LAST], LAST, 0, SLOTS, nc.scalar.copy)
+        for h in range(2):
+            interleave(q_in[LAST][:, h * SLOTS * 2 : (h + 1) * SLOTS * 2], LAST, h * SLOTS // 2, (h + 1) * SLOTS // 2, nc.scalar.copy)
         q_final = [tile(f"q_final_{h}", SLOTS * 2, BF16) for h in range(2)]
         for h in range(2):
             interleave(q_final[h], 2, h * SLOTS // 2, (h + 1) * SLOTS // 2, nc.scalar.copy)
@@ -197,11 +198,7 @@ def tile_moe_shr_lin_relu_kernel(tc, xT, w_words, w_scales, b, gate, offs, pos1,
         def shared_multiply(a, j):
             multiply(shared[j][:], E, a, s_codes[:, a * T + j * N : a * T + (j + 1) * N], s_scales[a][:, j * N : (j + 1) * N], a == 0, a == LAST)
 
-        for h in range(2):
-            shared_quantize(0, HALVES[h], s_first[h][:])
-            for j in (2 * h, 2 * h + 1):
-                shared_multiply(0, j)
-        for a in range(1, LAST):
+        for a in range(LAST):
             shared_quantize(a, whole, s_in[a])
             for j in range(T // N):
                 shared_multiply(a, j)

@@ -13,6 +13,8 @@ FP4X4 = mybir.dt.float4_e2m1fn_x4
 RELU = mybir.ActivationFunctionType.Relu
 COPY = mybir.ActivationFunctionType.Copy
 MULT = mybir.AluOpType.mult
+ADD = mybir.AluOpType.add
+MAX = mybir.AluOpType.max
 
 P = 128
 K, T, E, C, N = 2048, 512, 4, 256, 128
@@ -46,9 +48,8 @@ def tile_moe_shr_lin_relu_kernel(tc, xT, w_words, w_scales, b, gate, offs, pos1,
         b_sb = tile("b_sb", E + 1, F32)
         gate_sb = keep.tile([P, 2, T], F32, name="gate_sb")
         y_sb = tile("y_sb", SLOTS, F32)
-        ys_sb = tile("ys_sb", T, F32)
         banks = [psum.tile([P, C], F32, name=f"bank{e}", tag=f"bank{e}") for e in range(E)]
-        shared = [psum.tile([P, N], F32, name=f"shared{j}", tag=f"shared{j}") for j in range(T // N)]
+        shared = [psum.tile([P, HALF], F32, name=f"shared{h}", tag=f"shared{h}") for h in range(2)]
 
         x_rows = xT.rearrange("(a p t) w -> a p t w", p=P, t=4)
         again = tile("again", 2 * T, F32)
@@ -167,6 +168,9 @@ def tile_moe_shr_lin_relu_kernel(tc, xT, w_words, w_scales, b, gate, offs, pos1,
             interleave(q_final[h], 2, h * SLOTS // 2, (h + 1) * SLOTS // 2, nc.scalar.copy)
         shared_interleave(s_in[2], 2, whole, nc.scalar.copy)
 
+        floor = tile("floor", 1, F32, tag="gath_2")
+        nc.scalar.activation(floor[:], b_sb[:, E : E + 1], COPY, scale=-1.0)
+
         codes = {a: tile(f"codes_{a}", SLOTS, U32) for a in range(2)}
         codes[LAST] = tile("codes_last", SLOTS, U32, tag="gath_1")
         for a in SUM_ORDER[:-1]:
@@ -195,33 +199,29 @@ def tile_moe_shr_lin_relu_kernel(tc, xT, w_words, w_scales, b, gate, offs, pos1,
         def shared_quantize(a, cols, src):
             quantize(s_codes[:, a * T + cols.start : a * T + cols.stop], s_scales[a][:, cols], src)
 
-        def shared_multiply(a, j):
-            multiply(shared[j][:], E, a, s_codes[:, a * T + j * N : a * T + (j + 1) * N], s_scales[a][:, j * N : (j + 1) * N], a == 0, a == LAST)
+        def shared_multiply(a, h):
+            cols = HALVES[h]
+            multiply(shared[h][:], E, a, s_codes[:, a * T + cols.start : a * T + cols.stop], s_scales[a][:, cols], a == 0, a == LAST)
 
         for a in range(LAST):
             shared_quantize(a, whole, s_in[a])
-            for j in range(T // N):
-                shared_multiply(a, j)
+            for h in range(2):
+                shared_multiply(a, h)
 
-        def pick(dst, r, lst, cols):
-            nc.vector.tensor_tensor(dst, y_sb[:].indirect(lst[:, cols.start // 16 : cols.stop // 16]), gate_sb[:, r, cols], MULT)
-
-        first = tile("first", T, F32)
+        first = [tile("first_0", HALF, F32)[:], last_rows[0][:, 0:HALF]]
+        second = s_late[:, 0 : 4 * HALF].bitcast(F32)
+        gated = tile("gated", T, F32)
+        partial = [last_rows[0][:, HALF:T], tile("partial_1", HALF, F32)[:]]
         total = tile("total", T, F32)
-        pick(first[:], 0, pos1_sb, whole)
-        second = [tile("second_0", HALF, F32)[:]]
-        shared_quantize(LAST, HALVES[0], s_late[:, 0 : 4 * HALF])
-        pick(second[0], 1, pos2_sb, HALVES[0])
-        shared_quantize(LAST, HALVES[1], s_late[:, 4 * HALF :])
-        for j in range(T // N):
-            shared_multiply(LAST, j)
-            nc.scalar.activation(ys_sb[:, j * N : (j + 1) * N], shared[j][:], RELU, bias=b_sb[:, E : E + 1])
-        held = tile("held", HALF + T, F32, tag="last_row0")
-        second.append(held[:, 0:HALF])
-        partial = held[:, HALF:]
-        pick(second[1], 1, pos2_sb, HALVES[1])
         for h, cols in enumerate(HALVES):
-            nc.vector.tensor_add(partial[:, cols], first[:, cols], second[h])
-        for cols in HALVES:
-            nc.vector.tensor_add(total[:, cols], partial[:, cols], ys_sb[:, cols])
+            nc.vector.tensor_tensor(first[h], y_sb[:].indirect(pos1_sb[:, cols.start // 16 : cols.stop // 16]), gate_sb[:, 0, cols], MULT)
+            shared_quantize(LAST, cols, s_late[:, 4 * cols.start : 4 * cols.stop])
+        for h, cols in enumerate(HALVES):
+            nc.scalar.activation(second[:, cols], y_sb[:].indirect(pos2_sb[:, cols.start // 16 : cols.stop // 16]), COPY)
+            shared_multiply(LAST, h)
+        for h, cols in enumerate(HALVES):
+            nc.vector.scalar_tensor_tensor(partial[h], shared[h][:], floor[:], first[h], MAX, ADD)
+            nc.vector.tensor_mul(gated[:, cols], second[:, cols], gate_sb[:, 1, cols])
+        for h, cols in enumerate(HALVES):
+            nc.vector.scalar_tensor_tensor(total[:, cols], partial[h], b_sb[:, E : E + 1], gated[:, cols], ADD, ADD)
             nc.sync.dma_start(out[:, cols], total[:, cols])

@@ -24,7 +24,8 @@ LAST = PASSES - 1
 SLOTS = E * C
 HALF = T // 2
 HALVES = (slice(0, HALF), slice(HALF, T))
-SCALAR_SLOTS = 352
+SCALAR_SLOTS = 224
+GPSIMD_TOKENS = 192
 SCALAR_TOKENS = 128
 SUM_ORDER = (0, 1, LAST, 2)
 
@@ -86,14 +87,16 @@ def tile_moe_shr_lin_relu_kernel(tc, xT, w_words, w_scales, b, gate, offs, pos1,
         load_pair(2, 0, whole)
         load_last_row(1)
         load_last_row(3)
-        nc.sync.dma_start(w_sb[:].bitcast(I32), w_words.rearrange("e a p n -> p (e a) n").bitcast(I32))
-        scale_rows = w_scales.rearrange("e a q n -> q (e a) n").bitcast(I32)
-        for quad in range(4):
-            nc.sync.dma_start(ws_sb[32 * quad : 32 * quad + 4].bitcast(I32), scale_rows[4 * quad : 4 * quad + 4])
-        nc.sync.dma_start(b_sb[:], b)
-        nc.sync.dma_start(pos1_sb[:], pos1)
-        nc.sync.dma_start(pos2_sb[:], pos2)
-        nc.sync.dma_start(gate_sb[:], gate.rearrange("r n t -> n r t"))
+
+        def load_constants():
+            nc.sync.dma_start(w_sb[:].bitcast(I32), w_words.rearrange("e a p n -> p (e a) n").bitcast(I32))
+            scale_rows = w_scales.rearrange("e a q n -> q (e a) n").bitcast(I32)
+            for quad in range(4):
+                nc.sync.dma_start(ws_sb[32 * quad : 32 * quad + 4].bitcast(I32), scale_rows[4 * quad : 4 * quad + 4])
+            nc.sync.dma_start(b_sb[:], b)
+            nc.sync.dma_start(pos1_sb[:], pos1)
+            nc.sync.dma_start(pos2_sb[:], pos2)
+            nc.sync.dma_start(gate_sb[:], gate.rearrange("r n t -> n r t"))
 
         def plane_values(a, u, cols):
             return planes[a][:, u * T : (u + 1) * T].bitcast(BF16).rearrange("p (w e) -> p w e", e=2)[:, cols]
@@ -147,7 +150,11 @@ def tile_moe_shr_lin_relu_kernel(tc, xT, w_words, w_scales, b, gate, offs, pos1,
         gather_row(LAST, 1, last_rows[1], 0, SLOTS)
         for h in range(2):
             gather_row(LAST, 3, last_rows[3], h * SLOTS // 2, (h + 1) * SLOTS // 2)
-        nc.sync.dma_start(last_rows[0][:, T:], x_rows[LAST, :, 1:4].rearrange("p t w -> p (t w)"))
+        late_raw = [tile(f"late_raw{h}", 4 * HALF, F32) for h in range(2)]
+        for h, cols in enumerate(HALVES):
+            nc.sync.dma_start(late_raw[h][:].rearrange("p (t w) -> p t w", t=4), x_rows[LAST, :, :, cols])
+            if h == 0:
+                load_constants()
         for a in range(1, LAST):
             for u in (1, 0):
                 cast_pair(a, u, whole, nc.gpsimd.tensor_copy)
@@ -155,11 +162,12 @@ def tile_moe_shr_lin_relu_kernel(tc, xT, w_words, w_scales, b, gate, offs, pos1,
 
         q_early = tile("q_early", 2 * SLOTS * 4, BF16, tag="raw_2_0")
         q_in = {a: q_early[:, a * SLOTS * 4 : (a + 1) * SLOTS * 4] for a in range(2)}
+        s_in = {1: tile("s_in_1", T * 4, BF16)[:], 2: tile("s_in_2", T * 4, BF16)[:]}
+        shared_interleave(s_in[1][:, 0 : 4 * GPSIMD_TOKENS], 1, slice(0, GPSIMD_TOKENS), nc.gpsimd.tensor_copy)
         for a in range(2):
             interleave(q_in[a], a, 0, SLOTS, nc.gpsimd.tensor_copy)
-        s_in = {1: tile("s_in_1", T * 4, BF16)[:], 2: tile("s_in_2", T * 4, BF16)[:]}
         s_in[0] = s_first[:]
-        shared_interleave(s_in[1], 1, whole, nc.scalar.copy)
+        shared_interleave(s_in[1][:, 4 * GPSIMD_TOKENS :], 1, slice(GPSIMD_TOKENS, T), nc.scalar.copy)
         q_in[LAST] = tile("q_last", SLOTS * 4, BF16)[:]
         for h in range(2):
             interleave(q_in[LAST][:, h * SLOTS * 2 : (h + 1) * SLOTS * 2], LAST, h * SLOTS // 2, (h + 1) * SLOTS // 2, nc.scalar.copy)
@@ -168,8 +176,19 @@ def tile_moe_shr_lin_relu_kernel(tc, xT, w_words, w_scales, b, gate, offs, pos1,
             interleave(q_final[h], 2, h * SLOTS // 2, (h + 1) * SLOTS // 2, nc.scalar.copy)
         shared_interleave(s_in[2], 2, whole, nc.scalar.copy)
 
-        floor = tile("floor", 1, F32, tag="gath_2")
-        nc.scalar.activation(floor[:], b_sb[:, E : E + 1], COPY, scale=-1.0)
+        after_routed = tile("after_routed", 2 * HALF + 8, U32, tag="gath_2")
+        floor = after_routed[:, 2 * HALF : 2 * HALF + 1].bitcast(F32)
+        nc.scalar.activation(floor, b_sb[:, E : E + 1], COPY, scale=-1.0)
+
+        s_late = [after_routed[:, 0 : 2 * HALF].bitcast(BF16)]
+
+        def late_rows(h):
+            nc.scalar.copy(
+                s_late[h].rearrange("p (c i t) -> p c t i", i=2, t=4),
+                late_raw[h][:].rearrange("p (t c i) -> p c t i", t=4, i=2),
+            )
+
+        late_rows(0)
 
         codes = {a: tile(f"codes_{a}", SLOTS, U32) for a in range(2)}
         codes[LAST] = tile("codes_last", SLOTS, U32, tag="gath_1")
@@ -189,12 +208,8 @@ def tile_moe_shr_lin_relu_kernel(tc, xT, w_words, w_scales, b, gate, offs, pos1,
             nc.scalar.activation(y_sb[:, cols], banks[e][:], RELU, bias=b_sb[:, e : e + 1])
 
         s_codes = tile("s_codes", PASSES * T, U32, tag="q_final_0")
-        s_late = tile("s_late", T * 4, BF16, tag="raw_2_0")
-        for cols in HALVES:
-            nc.scalar.copy(
-                s_late[:, 4 * cols.start : 4 * cols.stop].rearrange("p (c i t) -> p c t i", i=2, t=4),
-                last_rows[0][:].rearrange("p (t w) -> p t w", t=4)[:, :, cols].rearrange("p t (c i) -> p c t i", i=2),
-            )
+        s_late.append(tile("s_late", HALF * 4, BF16, tag="raw_2_0")[:])
+        late_rows(1)
 
         def shared_quantize(a, cols, src):
             quantize(s_codes[:, a * T + cols.start : a * T + cols.stop], s_scales[a][:, cols], src)
@@ -208,19 +223,19 @@ def tile_moe_shr_lin_relu_kernel(tc, xT, w_words, w_scales, b, gate, offs, pos1,
             for h in range(2):
                 shared_multiply(a, h)
 
-        first = [tile("first_0", HALF, F32)[:], last_rows[0][:, 0:HALF]]
-        second = s_late[:, 0 : 4 * HALF].bitcast(F32)
+        first = tile("first", T, F32)
+        second = late_raw[1][:, HALF : HALF + T]
         gated = tile("gated", T, F32)
-        partial = [last_rows[0][:, HALF:T], tile("partial_1", HALF, F32)[:]]
+        partial = [late_raw[1][:, 0:HALF], tile("partial_1", HALF, F32)[:]]
         total = tile("total", T, F32)
-        for h, cols in enumerate(HALVES):
-            nc.vector.tensor_tensor(first[h], y_sb[:].indirect(pos1_sb[:, cols.start // 16 : cols.stop // 16]), gate_sb[:, 0, cols], MULT)
-            shared_quantize(LAST, cols, s_late[:, 4 * cols.start : 4 * cols.stop])
+        shared_quantize(LAST, HALVES[0], s_late[0])
+        nc.vector.tensor_tensor(first[:], y_sb[:].indirect(pos1_sb[:]), gate_sb[:, 0], MULT)
+        shared_quantize(LAST, HALVES[1], s_late[1])
         for h, cols in enumerate(HALVES):
             nc.scalar.activation(second[:, cols], y_sb[:].indirect(pos2_sb[:, cols.start // 16 : cols.stop // 16]), COPY)
             shared_multiply(LAST, h)
         for h, cols in enumerate(HALVES):
-            nc.vector.scalar_tensor_tensor(partial[h], shared[h][:], floor[:], first[h], MAX, ADD)
+            nc.vector.scalar_tensor_tensor(partial[h], shared[h][:], floor, first[:, cols], MAX, ADD)
             nc.vector.tensor_mul(gated[:, cols], second[:, cols], gate_sb[:, 1, cols])
         for h, cols in enumerate(HALVES):
             nc.vector.scalar_tensor_tensor(total[:, cols], partial[h], b_sb[:, E : E + 1], gated[:, cols], ADD, ADD)

@@ -25,7 +25,7 @@ SLOTS = E * C
 HALF = T // 2
 HALVES = (slice(0, HALF), slice(HALF, T))
 SCALAR_SLOTS = 224
-GPSIMD_TOKENS = 192
+GPSIMD_TOKENS = 320
 SCALAR_TOKENS = 128
 SUM_ORDER = (0, 1, LAST, 2)
 
@@ -95,7 +95,6 @@ def tile_moe_shr_lin_relu_kernel(tc, xT, w_words, w_scales, b, gate, offs, pos1,
                 nc.sync.dma_start(ws_sb[32 * quad : 32 * quad + 4].bitcast(I32), scale_rows[4 * quad : 4 * quad + 4])
             nc.sync.dma_start(b_sb[:], b)
             nc.sync.dma_start(pos1_sb[:], pos1)
-            nc.sync.dma_start(pos2_sb[:], pos2)
             nc.sync.dma_start(gate_sb[:], gate.rearrange("r n t -> n r t"))
 
         def plane_values(a, u, cols):
@@ -155,6 +154,7 @@ def tile_moe_shr_lin_relu_kernel(tc, xT, w_words, w_scales, b, gate, offs, pos1,
             nc.sync.dma_start(late_raw[h][:].rearrange("p (t w) -> p t w", t=4), x_rows[LAST, :, :, cols])
             if h == 0:
                 load_constants()
+        nc.sync.dma_start(pos2_sb[:], pos2)
         for a in range(1, LAST):
             for u in (1, 0):
                 cast_pair(a, u, whole, nc.gpsimd.tensor_copy)
@@ -224,7 +224,7 @@ def tile_moe_shr_lin_relu_kernel(tc, xT, w_words, w_scales, b, gate, offs, pos1,
                 shared_multiply(a, h)
 
         first = tile("first", T, F32)
-        second = late_raw[1][:, HALF : HALF + T]
+        second = tile("second", T, F32)
         gated = tile("gated", T, F32)
         partial = [late_raw[1][:, 0:HALF], tile("partial_1", HALF, F32)[:]]
         total = tile("total", T, F32)

@@ -24,9 +24,10 @@ LAST = PASSES - 1
 SLOTS = E * C
 HALF = T // 2
 HALVES = (slice(0, HALF), slice(HALF, T))
-SCALAR_SLOTS = 224
-GPSIMD_TOKENS = 320
+SCALAR_SLOTS = 288
+GPSIMD_TOKENS = 288
 SCALAR_TOKENS = 128
+SECOND_PARTS = ((slice(0, 256), slice(256, 384)), (slice(384, T),))
 SUM_ORDER = (0, 1, LAST, 2)
 
 FLOPS = 2 * K * N * (SLOTS + T)
@@ -232,11 +233,11 @@ def tile_moe_shr_lin_relu_kernel(tc, xT, w_words, w_scales, b, gate, offs, pos1,
         nc.vector.tensor_tensor(first[:], y_sb[:].indirect(pos1_sb[:]), gate_sb[:, 0], MULT)
         shared_quantize(LAST, HALVES[1], s_late[1])
         for h, cols in enumerate(HALVES):
-            nc.scalar.activation(second[:, cols], y_sb[:].indirect(pos2_sb[:, cols.start // 16 : cols.stop // 16]), COPY)
             shared_multiply(LAST, h)
-        for h, cols in enumerate(HALVES):
             nc.vector.scalar_tensor_tensor(partial[h], shared[h][:], floor, first[:, cols], MAX, ADD)
-            nc.vector.tensor_mul(gated[:, cols], second[:, cols], gate_sb[:, 1, cols])
+            for part in SECOND_PARTS[h]:
+                nc.scalar.activation(second[:, part], y_sb[:].indirect(pos2_sb[:, part.start // 16 : part.stop // 16]), COPY)
+                nc.vector.tensor_mul(gated[:, part], second[:, part], gate_sb[:, 1, part])
         for h, cols in enumerate(HALVES):
             nc.vector.scalar_tensor_tensor(total[:, cols], partial[h], b_sb[:, E : E + 1], gated[:, cols], ADD, ADD)
             nc.sync.dma_start(out[:, cols], total[:, cols])

@@ -40,15 +40,15 @@ def tile_moe_shr_lin_relu_kernel(tc, xT, w_words, w_scales, b, gate, offs, pos1,
         psum = ctx.enter_context(tc.psum_pool(name="psum", bufs=1))
 
         def tile(name, width, dtype, tag=None):
-            return keep.tile([P, width], dtype, name=name, tag=tag or name, align_bytes=64)
+            return keep.tile([P, width], dtype, name=name, tag=tag or name, align_bytes=256)
 
         offs_sb = tile("offs_sb", SLOTS // 16, U16)
         pos1_sb = tile("pos1_sb", T // 16, U16)
         pos2_sb = tile("pos2_sb", T // 16, U16)
-        w_sb = keep.tile([P, (E + 1) * PASSES, 2 * N], U8, name="w_sb", align_bytes=64)
-        ws_sb = keep.tile([P, (E + 1) * PASSES, N], U8, name="ws_sb", align_bytes=64)
+        w_sb = keep.tile([P, (E + 1) * PASSES, 2 * N], U8, name="w_sb", align_bytes=256)
+        ws_sb = keep.tile([P, (E + 1) * PASSES, N], U8, name="ws_sb", align_bytes=256)
         b_sb = tile("b_sb", E + 1, F32)
-        gate_sb = keep.tile([P, 2, T], F32, name="gate_sb")
+        gate_sb = keep.tile([P, 2, T], F32, name="gate_sb", align_bytes=256)
         y_sb = tile("y_sb", SLOTS, F32)
         banks = [psum.tile([P, C], F32, name=f"bank{e}", tag=f"bank{e}") for e in range(E)]
         shared = [psum.tile([P, HALF], F32, name=f"shared{h}", tag=f"shared{h}") for h in range(2)]

@@ -85,18 +85,15 @@ def tile_moe_shr_lin_relu_kernel(tc, xT, w_words, w_scales, b, gate, offs, pos1,
         load_pair(1, 0, whole)
         load_pair(2, 1, whole)
         nc.sync.dma_start(again[:, 0:T], x_rows[0, :, 3])
-        load_pair(2, 0, whole)
         load_last_row(1)
+        load_pair(2, 0, whole)
         load_last_row(3)
 
-        def load_constants():
+        def load_weights():
             nc.sync.dma_start(w_sb[:].bitcast(I32), w_words.rearrange("e a p n -> p (e a) n").bitcast(I32))
             scale_rows = w_scales.rearrange("e a q n -> q (e a) n").bitcast(I32)
             for quad in range(4):
                 nc.sync.dma_start(ws_sb[32 * quad : 32 * quad + 4].bitcast(I32), scale_rows[4 * quad : 4 * quad + 4])
-            nc.sync.dma_start(b_sb[:], b)
-            nc.sync.dma_start(pos1_sb[:], pos1)
-            nc.sync.dma_start(gate_sb[:], gate.rearrange("r n t -> n r t"))
 
         def plane_values(a, u, cols):
             return planes[a][:, u * T : (u + 1) * T].bitcast(BF16).rearrange("p (w e) -> p w e", e=2)[:, cols]
@@ -151,10 +148,13 @@ def tile_moe_shr_lin_relu_kernel(tc, xT, w_words, w_scales, b, gate, offs, pos1,
         for h in range(2):
             gather_row(LAST, 3, last_rows[3], h * SLOTS // 2, (h + 1) * SLOTS // 2)
         late_raw = [tile(f"late_raw{h}", 4 * HALF, F32) for h in range(2)]
+        load_weights()
         for h, cols in enumerate(HALVES):
             nc.sync.dma_start(late_raw[h][:].rearrange("p (t w) -> p t w", t=4), x_rows[LAST, :, :, cols])
             if h == 0:
-                load_constants()
+                nc.sync.dma_start(b_sb[:], b)
+                nc.sync.dma_start(pos1_sb[:], pos1)
+                nc.sync.dma_start(gate_sb[:], gate.rearrange("r n t -> n r t"))
         nc.sync.dma_start(pos2_sb[:], pos2)
         for a in range(1, LAST):
             for u in (1, 0):

@@ -24,8 +24,8 @@ LAST = PASSES - 1
 SLOTS = E * C
 HALF = T // 2
 HALVES = (slice(0, HALF), slice(HALF, T))
-SCALAR_SLOTS = 288
-GPSIMD_TOKENS = 288
+SCALAR_SLOTS = 320
+GPSIMD_TOKENS = 256
 SCALAR_TOKENS = 128
 SECOND_PARTS = ((slice(0, 256), slice(256, 384)), (slice(384, T),))
 SUM_ORDER = (0, 1, LAST, 2)
@@ -56,7 +56,10 @@ def tile_moe_shr_lin_relu_kernel(tc, xT, w_words, w_scales, b, gate, offs, pos1,
         x_rows = xT.rearrange("(a p t) w -> a p t w", p=P, t=4)
         again = tile("again", 2 * T, F32)
         last_rows = [tile(f"last_row{t}", 4 * T, F32) for t in range(4)]
-        raw = {(a, u): tile(f"raw_{a}_{u}", 2 * T, F32) for a in range(LAST) for u in range(2)}
+        raw = {(a, u): tile(f"raw_{a}_{u}", 2 * T, F32)[:] for a in range(LAST) for u in range(2) if (a, u) != (1, 1)}
+        first_and_third = tile("first_and_third", 3 * T, U32)
+        raw[1, 1] = first_and_third[:, T:].bitcast(F32)
+        s_first = first_and_third[:, 0 : 2 * T].bitcast(BF16)
         planes = [tile(f"planes_{a}", 4 * T, U32) for a in range(LAST)]
         gath = [tile(f"gath_{a}", 2 * SLOTS, U32) for a in range(PASSES)]
         scales = [tile(f"scales_{a}", SLOTS, U8) for a in range(PASSES)]
@@ -65,7 +68,7 @@ def tile_moe_shr_lin_relu_kernel(tc, xT, w_words, w_scales, b, gate, offs, pos1,
         nc.vector.memset(ws_sb[:].rearrange("p g n -> p (g n)").bitcast(I32), 0)
 
         def raw_pair(a, u, cols):
-            return raw[a, u][:].rearrange("p (e w) -> p e w", e=2)[:, :, cols]
+            return raw[a, u].rearrange("p (e w) -> p e w", e=2)[:, :, cols]
 
         def load_pair(a, u, cols):
             nc.sync.dma_start(raw_pair(a, u, cols), x_rows[a, :, 2 * u : 2 * u + 2, cols])
@@ -80,7 +83,8 @@ def tile_moe_shr_lin_relu_kernel(tc, xT, w_words, w_scales, b, gate, offs, pos1,
         for cols in HALVES:
             load_pair(0, 0, cols)
         load_last_row(0)
-        load_pair(1, 1, whole)
+        for cols in HALVES:
+            load_pair(1, 1, cols)
         load_last_row(2)
         load_pair(1, 0, whole)
         load_pair(2, 1, whole)
@@ -105,9 +109,9 @@ def tile_moe_shr_lin_relu_kernel(tc, xT, w_words, w_scales, b, gate, offs, pos1,
             window = planes[a][:, u * T : (u + 3) * T]
             nc.vector.tensor_copy(gath[a][:, u * SLOTS + lo : (u + 1) * SLOTS], window.indirect(offs_sb[:, lo // 16 :]))
 
-        def gather_row(a, t, row_tile, lo, hi):
+        def gather_row(a, t, row, lo, hi):
             words = gath[a][:, t // 2 * SLOTS + lo : t // 2 * SLOTS + hi].bitcast(BF16).rearrange("p (n e) -> p n e", e=2)
-            nc.scalar.activation(words[:, :, t % 2], row_tile[:].indirect(offs_sb[:, lo // 16 : hi // 16]), COPY)
+            nc.scalar.activation(words[:, :, t % 2], row.indirect(offs_sb[:, lo // 16 : hi // 16]), COPY)
 
         def interleave(dst, a, lo, hi, copy):
             copy(dst[:].bitcast(U32).rearrange("p (n u) -> p n u", u=2), gath[a][:].rearrange("p (u n) -> p n u", u=2)[:, lo:hi])
@@ -138,15 +142,17 @@ def tile_moe_shr_lin_relu_kernel(tc, xT, w_words, w_scales, b, gate, offs, pos1,
         for cols, copy in zip(HALVES, (nc.gpsimd.tensor_copy, nc.scalar.copy)):
             cast_pair(0, 0, cols, copy)
         gather_pair(0, 0, 0)
-        s_first = tile("s_first", 4 * T, BF16)
+        shared_interleave(s_first[:, 0 : 4 * HALF], 0, HALVES[0], nc.gpsimd.tensor_copy)
         for cols in HALVES:
-            shared_interleave(s_first[:, 4 * cols.start : 4 * cols.stop], 0, cols, nc.gpsimd.tensor_copy)
+            cast_pair(1, 1, cols, nc.gpsimd.tensor_copy)
+        gather_pair(1, 1, 0)
+        shared_interleave(s_first[:, 4 * HALF :], 0, HALVES[1], nc.gpsimd.tensor_copy)
         for t in (0, 2):
-            gather_row(LAST, t, last_rows[t], 0, SLOTS)
-        gather_row(0, 3, again, 0, SCALAR_SLOTS)
-        gather_row(LAST, 1, last_rows[1], 0, SLOTS)
+            gather_row(LAST, t, last_rows[t][:], 0, SLOTS)
+        gather_row(0, 3, again[:], 0, SCALAR_SLOTS)
+        gather_row(LAST, 1, last_rows[1][:], 0, SLOTS)
         for h in range(2):
-            gather_row(LAST, 3, last_rows[3], h * SLOTS // 2, (h + 1) * SLOTS // 2)
+            gather_row(LAST, 3, last_rows[3][:], h * SLOTS // 2, (h + 1) * SLOTS // 2)
         late_raw = [tile(f"late_raw{h}", 4 * HALF, F32) for h in range(2)]
         load_weights()
         for h, cols in enumerate(HALVES):
@@ -156,10 +162,9 @@ def tile_moe_shr_lin_relu_kernel(tc, xT, w_words, w_scales, b, gate, offs, pos1,
                 nc.sync.dma_start(pos1_sb[:], pos1)
                 nc.sync.dma_start(gate_sb[:], gate.rearrange("r n t -> n r t"))
         nc.sync.dma_start(pos2_sb[:], pos2)
-        for a in range(1, LAST):
-            for u in (1, 0):
-                cast_pair(a, u, whole, nc.gpsimd.tensor_copy)
-                gather_pair(a, u, 0)
+        for a, u in ((1, 0), (2, 1), (2, 0)):
+            cast_pair(a, u, whole, nc.gpsimd.tensor_copy)
+            gather_pair(a, u, 0)
 
         q_early = tile("q_early", 2 * SLOTS * 4, BF16, tag="raw_2_0")
         q_in = {a: q_early[:, a * SLOTS * 4 : (a + 1) * SLOTS * 4] for a in range(2)}
@@ -167,7 +172,7 @@ def tile_moe_shr_lin_relu_kernel(tc, xT, w_words, w_scales, b, gate, offs, pos1,
         shared_interleave(s_in[1][:, 0 : 4 * GPSIMD_TOKENS], 1, slice(0, GPSIMD_TOKENS), nc.gpsimd.tensor_copy)
         for a in range(2):
             interleave(q_in[a], a, 0, SLOTS, nc.gpsimd.tensor_copy)
-        s_in[0] = s_first[:]
+        s_in[0] = s_first
         shared_interleave(s_in[1][:, 4 * GPSIMD_TOKENS :], 1, slice(GPSIMD_TOKENS, T), nc.scalar.copy)
         q_in[LAST] = tile("q_last", SLOTS * 4, BF16)[:]
         for h in range(2):

from contextlib import ExitStack

import concourse.mybir as mybir

F32 = mybir.dt.float32
BF16 = mybir.dt.bfloat16
U32 = mybir.dt.uint32
I32 = mybir.dt.int32
U16 = mybir.dt.uint16
U8 = mybir.dt.uint8
FP8X4 = mybir.dt.float8_e4m3fn_x4
FP4X4 = mybir.dt.float4_e2m1fn_x4
RELU = mybir.ActivationFunctionType.Relu
COPY = mybir.ActivationFunctionType.Copy
MULT = mybir.AluOpType.mult
ADD = mybir.AluOpType.add
MAX = mybir.AluOpType.max

P = 128
K, T, E, C, N = 2048, 512, 4, 256, 128
K_PASS = 512
PASSES = K // K_PASS
LAST = PASSES - 1
SLOTS = E * C
HALF = T // 2
HALVES = (slice(0, HALF), slice(HALF, T))
SCALAR_SLOTS = 320
GPSIMD_TOKENS = 256
SCALAR_TOKENS = 128
SECOND_PARTS = ((slice(0, 256), slice(256, 384)), (slice(384, T),))
SUM_ORDER = (0, 1, LAST, 2)

FLOPS = 2 * K * N * (SLOTS + T)


def tile_moe_shr_lin_relu_kernel(tc, xT, w_words, w_scales, b, gate, offs, pos1, pos2, out):
    nc = tc.nc
    with ExitStack() as ctx:
        keep = ctx.enter_context(tc.tile_pool(name="keep", bufs=1))
        psum = ctx.enter_context(tc.psum_pool(name="psum", bufs=1))

        def tile(name, width, dtype, tag=None):
            return keep.tile([P, width], dtype, name=name, tag=tag or name, align_bytes=256)

        offs_sb = tile("offs_sb", SLOTS // 16, U16)
        pos1_sb = tile("pos1_sb", T // 16, U16)
        pos2_sb = tile("pos2_sb", T // 16, U16)
        w_sb = keep.tile([P, (E + 1) * PASSES, 2 * N], U8, name="w_sb", align_bytes=256)
        ws_sb = keep.tile([P, (E + 1) * PASSES, N], U8, name="ws_sb", align_bytes=256)
        b_sb = tile("b_sb", E + 1, F32)
        gate_sb = keep.tile([P, 2, T], F32, name="gate_sb", align_bytes=256)
        y_sb = tile("y_sb", SLOTS, F32)
        banks = [psum.tile([P, C], F32, name=f"bank{e}", tag=f"bank{e}") for e in range(E)]
        shared = [psum.tile([P, HALF], F32, name=f"shared{h}", tag=f"shared{h}") for h in range(2)]

        x_rows = xT.rearrange("(a p t) w -> a p t w", p=P, t=4)
        again = tile("again", 2 * T, F32)
        last_rows = [tile(f"last_row{t}", 4 * T, F32) for t in range(4)]
        raw = {(a, u): tile(f"raw_{a}_{u}", 2 * T, F32)[:] for a in range(LAST) for u in range(2) if (a, u) != (1, 1)}
        first_and_third = tile("first_and_third", 3 * T, U32)
        raw[1, 1] = first_and_third[:, T:].bitcast(F32)
        s_first = first_and_third[:, 0 : 2 * T].bitcast(BF16)
        planes = [tile(f"planes_{a}", 4 * T, U32) for a in range(LAST)]
        gath = [tile(f"gath_{a}", 2 * SLOTS, U32) for a in range(PASSES)]
        scales = [tile(f"scales_{a}", SLOTS, U8) for a in range(PASSES)]
        s_scales = [tile(f"s_scales_{a}", T, U8) for a in range(PASSES)]

        nc.vector.memset(ws_sb[:].rearrange("p g n -> p (g n)").bitcast(I32), 0)

        def raw_pair(a, u, cols):
            return raw[a, u].rearrange("p (e w) -> p e w", e=2)[:, :, cols]

        def load_pair(a, u, cols):
            nc.sync.dma_start(raw_pair(a, u, cols), x_rows[a, :, 2 * u : 2 * u + 2, cols])

        def load_last_row(t):
            nc.sync.dma_start(last_rows[t][:, 0:T], x_rows[LAST, :, t])

        whole = slice(0, T)
        for cols in HALVES:
            load_pair(0, 1, cols)
        nc.sync.dma_start(offs_sb[:], offs)
        for cols in HALVES:
            load_pair(0, 0, cols)
        load_last_row(0)
        for cols in HALVES:
            load_pair(1, 1, cols)
        load_last_row(2)
        load_pair(1, 0, whole)
        load_pair(2, 1, whole)
        nc.sync.dma_start(again[:, 0:T], x_rows[0, :, 3])
        load_last_row(1)
        load_pair(2, 0, whole)
        load_last_row(3)

        def load_weights():
            nc.sync.dma_start(w_sb[:].bitcast(I32), w_words.rearrange("e a p n -> p (e a) n").bitcast(I32))
            scale_rows = w_scales.rearrange("e a q n -> q (e a) n").bitcast(I32)
            for quad in range(4):
                nc.sync.dma_start(ws_sb[32 * quad : 32 * quad + 4].bitcast(I32), scale_rows[4 * quad : 4 * quad + 4])

        def plane_values(a, u, cols):
            return planes[a][:, u * T : (u + 1) * T].bitcast(BF16).rearrange("p (w e) -> p w e", e=2)[:, cols]

        def cast_pair(a, u, cols, copy):
            copy(plane_values(a, u, cols), raw_pair(a, u, cols).rearrange("p e w -> p w e"))

        def gather_pair(a, u, lo):
            window = planes[a][:, u * T : (u + 3) * T]
            nc.vector.tensor_copy(gath[a][:, u * SLOTS + lo : (u + 1) * SLOTS], window.indirect(offs_sb[:, lo // 16 :]))

        def gather_row(a, t, row, lo, hi):
            words = gath[a][:, t // 2 * SLOTS + lo : t // 2 * SLOTS + hi].bitcast(BF16).rearrange("p (n e) -> p n e", e=2)
            nc.scalar.activation(words[:, :, t % 2], row.indirect(offs_sb[:, lo // 16 : hi // 16]), COPY)

        def interleave(dst, a, lo, hi, copy):
            copy(dst[:].bitcast(U32).rearrange("p (n u) -> p n u", u=2), gath[a][:].rearrange("p (u n) -> p n u", u=2)[:, lo:hi])

        def shared_interleave(dst, a, cols, copy):
            words = planes[a][:, 0 : 2 * T].rearrange("p (u w) -> p w u", u=2)
            copy(dst.bitcast(U32).rearrange("p (w u) -> p w u", u=2), words[:, cols])

        def quantize(dst, plane, src):
            nc.vector.quantize_mx(out=dst.bitcast(FP8X4), scales=plane, in_=src)

        def multiply(acc, e, a, words, plane, start, stop):
            nc.tensor.matmul_mx(
                out=acc,
                lhsT=w_sb[:, e * PASSES + a, :].bitcast(FP4X4),
                lhsT_scale=ws_sb[:, e * PASSES + a, :],
                rhs=words.bitcast(FP8X4),
                rhs_scale=plane,
                start=start,
                stop=stop,
            )

        for cols in HALVES:
            cast_pair(0, 1, slice(cols.start, cols.start + SCALAR_TOKENS), nc.scalar.copy)
            cast_pair(0, 1, slice(cols.start + SCALAR_TOKENS, cols.stop), nc.vector.tensor_copy)
        gather_row(0, 2, raw[0, 1], 0, SCALAR_SLOTS)
        gather_pair(0, 1, SCALAR_SLOTS)
        for cols, copy in zip(HALVES, (nc.gpsimd.tensor_copy, nc.scalar.copy)):
            cast_pair(0, 0, cols, copy)
        gather_pair(0, 0, 0)
        shared_interleave(s_first[:, 0 : 4 * HALF], 0, HALVES[0], nc.gpsimd.tensor_copy)
        for cols in HALVES:
            cast_pair(1, 1, cols, nc.gpsimd.tensor_copy)
        gather_pair(1, 1, 0)
        shared_interleave(s_first[:, 4 * HALF :], 0, HALVES[1], nc.gpsimd.tensor_copy)
        for t in (0, 2):
            gather_row(LAST, t, last_rows[t][:], 0, SLOTS)
        gather_row(0, 3, again[:], 0, SCALAR_SLOTS)
        gather_row(LAST, 1, last_rows[1][:], 0, SLOTS)
        for h in range(2):
            gather_row(LAST, 3, last_rows[3][:], h * SLOTS // 2, (h + 1) * SLOTS // 2)
        late_raw = [tile(f"late_raw{h}", 4 * HALF, F32) for h in range(2)]
        load_weights()
        for h, cols in enumerate(HALVES):
            nc.sync.dma_start(late_raw[h][:].rearrange("p (t w) -> p t w", t=4), x_rows[LAST, :, :, cols])
            if h == 0:
                nc.sync.dma_start(b_sb[:], b)
                nc.sync.dma_start(pos1_sb[:], pos1)
                nc.sync.dma_start(gate_sb[:], gate.rearrange("r n t -> n r t"))
        nc.sync.dma_start(pos2_sb[:], pos2)
        for a, u in ((1, 0), (2, 1), (2, 0)):
            cast_pair(a, u, whole, nc.gpsimd.tensor_copy)
            gather_pair(a, u, 0)

        q_early = tile("q_early", 2 * SLOTS * 4, BF16, tag="raw_2_0")
        q_in = {a: q_early[:, a * SLOTS * 4 : (a + 1) * SLOTS * 4] for a in range(2)}
        s_in = {1: tile("s_in_1", T * 4, BF16)[:], 2: tile("s_in_2", T * 4, BF16)[:]}
        shared_interleave(s_in[1][:, 0 : 4 * GPSIMD_TOKENS], 1, slice(0, GPSIMD_TOKENS), nc.gpsimd.tensor_copy)
        for a in range(2):
            interleave(q_in[a], a, 0, SLOTS, nc.gpsimd.tensor_copy)
        s_in[0] = s_first
        shared_interleave(s_in[1][:, 4 * GPSIMD_TOKENS :], 1, slice(GPSIMD_TOKENS, T), nc.scalar.copy)
        q_in[LAST] = tile("q_last", SLOTS * 4, BF16)[:]
        for h in range(2):
            interleave(q_in[LAST][:, h * SLOTS * 2 : (h + 1) * SLOTS * 2], LAST, h * SLOTS // 2, (h + 1) * SLOTS // 2, nc.scalar.copy)
        q_final = [tile(f"q_final_{h}", SLOTS * 2, BF16) for h in range(2)]
        for h in range(2):
            interleave(q_final[h], 2, h * SLOTS // 2, (h + 1) * SLOTS // 2, nc.scalar.copy)
        shared_interleave(s_in[2], 2, whole, nc.scalar.copy)

        after_routed = tile("after_routed", 2 * HALF + 8, U32, tag="gath_2")
        floor = after_routed[:, 2 * HALF : 2 * HALF + 1].bitcast(F32)
        nc.scalar.activation(floor, b_sb[:, E : E + 1], COPY, scale=-1.0)

        s_late = [after_routed[:, 0 : 2 * HALF].bitcast(BF16)]

        def late_rows(h):
            nc.scalar.copy(
                s_late[h].rearrange("p (c i t) -> p c t i", i=2, t=4),
                late_raw[h][:].rearrange("p (t c i) -> p c t i", t=4, i=2),
            )

        late_rows(0)

        codes = {a: tile(f"codes_{a}", SLOTS, U32) for a in range(2)}
        codes[LAST] = tile("codes_last", SLOTS, U32, tag="gath_1")
        for a in SUM_ORDER[:-1]:
            quantize(codes[a][:], scales[a][:], q_in[a])
            for e in range(E):
                cols = slice(e * C, (e + 1) * C)
                multiply(banks[e][:], e, a, codes[a][:, cols], scales[a][:, cols], a == SUM_ORDER[0], False)
        a = SUM_ORDER[-1]
        codes[a] = tile("codes_closing", SLOTS, U32, tag="raw_2_0")
        for e in range(E):
            cols = slice(e * C, (e + 1) * C)
            if e % 2 == 0:
                both = slice(e * C, (e + 2) * C)
                quantize(codes[a][:, both], scales[a][:, both], q_final[e // 2][:])
            multiply(banks[e][:], e, a, codes[a][:, cols], scales[a][:, cols], False, True)
            nc.scalar.activation(y_sb[:, cols], banks[e][:], RELU, bias=b_sb[:, e : e + 1])

        s_codes = tile("s_codes", PASSES * T, U32, tag="q_final_0")
        s_late.append(tile("s_late", HALF * 4, BF16, tag="raw_2_0")[:])
        late_rows(1)

        def shared_quantize(a, cols, src):
            quantize(s_codes[:, a * T + cols.start : a * T + cols.stop], s_scales[a][:, cols], src)

        def shared_multiply(a, h):
            cols = HALVES[h]
            multiply(shared[h][:], E, a, s_codes[:, a * T + cols.start : a * T + cols.stop], s_scales[a][:, cols], a == 0, a == LAST)

        for a in range(LAST):
            shared_quantize(a, whole, s_in[a])
            for h in range(2):
                shared_multiply(a, h)

        first = tile("first", T, F32)
        second = tile("second", T, F32)
        gated = tile("gated", T, F32)
        partial = [late_raw[1][:, 0:HALF], tile("partial_1", HALF, F32)[:]]
        total = tile("total", T, F32)
        shared_quantize(LAST, HALVES[0], s_late[0])
        nc.vector.tensor_tensor(first[:], y_sb[:].indirect(pos1_sb[:]), gate_sb[:, 0], MULT)
        shared_quantize(LAST, HALVES[1], s_late[1])
        for h, cols in enumerate(HALVES):
            shared_multiply(LAST, h)
            nc.vector.scalar_tensor_tensor(partial[h], shared[h][:], floor, first[:, cols], MAX, ADD)
            for part in SECOND_PARTS[h]:
                nc.scalar.activation(second[:, part], y_sb[:].indirect(pos2_sb[:, part.start // 16 : part.stop // 16]), COPY)
                nc.vector.tensor_mul(gated[:, part], second[:, part], gate_sb[:, 1, part])
        for h, cols in enumerate(HALVES):
            nc.vector.scalar_tensor_tensor(total[:, cols], partial[h], b_sb[:, E : E + 1], gated[:, cols], ADD, ADD)
            nc.sync.dma_start(out[:, cols], total[:, cols])
